import numpy as np
import ml_dtypes


def mxq(x, axis, fmt="e4m3"):
    dtype, down = {"e4m3": (ml_dtypes.float8_e4m3fn, 7), "e5m2": (ml_dtypes.float8_e5m2, 14)}[fmt]
    v = np.moveaxis(np.asarray(x, np.float32).astype(ml_dtypes.bfloat16).astype(np.float64), axis, -1)
    blocks = v.reshape(v.shape[:-1] + (-1, 32))
    amax = np.abs(blocks).max(-1, keepdims=True)
    byte = np.maximum(np.where(amax > 0, np.frexp(amax)[1] - 1 + 127, 0) - down, 1)
    scale = np.exp2(byte - 127.0)
    codes = (blocks / scale).astype(np.float32).astype(dtype).astype(np.float64)
    return np.moveaxis((codes * scale).reshape(v.shape), -1, axis)


WIDE = False


def mx_kscale(k):
    if not WIDE:
        return np.ones(k)
    levels = np.array([10, -10, 5, -5, 0])
    if k % 512:
        return np.exp2(np.random.permutation(np.resize(levels, k // 32))).repeat(32)
    a = np.empty((k // 512, 16))
    for p in range(k // 512):
        a[p, :8] = np.random.permutation(np.resize(levels, 8))
        for g in range(8):
            far = levels[np.abs(levels - a[p, g]) >= 10]
            a[p, g + 8] = far[np.random.randint(len(far))]
    return np.exp2(a.ravel()).repeat(32)


def f64(x):
    return np.asarray(x).astype(np.float64)


def striped(idx):
    return np.tile(idx.reshape(-1, 16).T, (8, 1)).astype(np.uint16)


def unstriped(offs):
    return offs[:16].T.reshape(-1).astype(np.int64)


E2M1 = np.array([0.0, 0.5, 1.0, 1.5, 2.0, 3.0, 4.0, 6.0, -0.0, -0.5, -1.0, -1.5, -2.0, -3.0, -4.0, -6.0])


def pack_weight(w, fmt):
    k, n = w.shape
    w = f64(np.asarray(w, np.float32).astype(ml_dtypes.bfloat16)).reshape(k // 32, 32, n)
    amax = np.abs(w).max(1)
    if fmt == "e4m3":
        byte = np.frexp(amax)[1] - 1 + 127 - 7
    else:
        mant, ex = np.frexp(amax / 6.0)
        byte = np.where(mant > 0.5, ex, ex - 1) + 127
    byte = np.clip(np.where(amax > 0, byte, 1), 1, 254)
    scaled = (w * np.exp2(127.0 - byte)[:, None, :]).reshape(k, n).astype(np.float32)
    by_word = np.ascontiguousarray(scaled.reshape(k // 512, 128, 4, n).transpose(0, 1, 3, 2))
    if fmt == "e4m3":
        words = by_word.astype(ml_dtypes.float8_e4m3fn).view(np.uint8)
    else:
        c = by_word.astype(ml_dtypes.float4_e2m1fn).view(np.uint8) & 0xF
        words = (c[..., 0::2] | (c[..., 1::2] << 4)).reshape(k // 512, 128, 2 * n)
    return np.ascontiguousarray(words), np.ascontiguousarray(byte.astype(np.uint8).reshape(k // 512, 16, n))


def unpack_weight(words, scales, fmt):
    g, _, n = scales.shape
    words = np.ascontiguousarray(words).reshape(g, 128, n, -1)
    if fmt == "e4m3":
        vals = words.view(ml_dtypes.float8_e4m3fn).astype(np.float64)
    else:
        nib = np.empty((g, 128, n, 4), np.uint8)
        nib[..., 0::2] = words & 0xF
        nib[..., 1::2] = words >> 4
        vals = E2M1[nib]
    vals = vals * np.repeat(np.exp2(scales.astype(np.float64) - 127.0), 8, axis=1)[..., None]
    return vals.transpose(0, 1, 3, 2).reshape(g * 512, n)


def gelu(v):
    return 0.5 * v * (1.0 + np.tanh(np.sqrt(2.0 / np.pi) * (v + 0.044715 * v**3)))


def bf(x):
    return np.asarray(x, np.float32).astype(ml_dtypes.bfloat16)

def planes(Y):
    n, m = Y.shape
    b = f64(bf(Y)).reshape(n // 32, 32, m)
    amax = np.abs(b).max(1)
    byte = np.clip(np.where(amax > 0, np.frexp(amax)[1] - 1 + 127 - 7, 1), 1, 254)
    codes = (b * np.exp2(127.0 - byte)[:, None, :]).reshape(n, m).astype(np.float32).astype(ml_dtypes.float8_e4m3fn).view(np.uint8)
    words = codes.reshape(n // 512, 128, 4, m).transpose(0, 1, 3, 2)
    return np.ascontiguousarray(words), np.ascontiguousarray(byte.astype(np.uint8).reshape(n // 512, 16, m))


K, T, S, H, N = 1024, 2048, 1024, 512, 1024

def setup_inputs():
    n = np.random.standard_normal
    s = mx_kscale(K)[:, None]
    u = mx_kscale(H)[:, None]
    amp = np.exp(0.8 * n(N))
    tab_words, tab_scales = pack_weight(n((K, T)) * s, "e4m3")
    w1_words, w1_scales = pack_weight(n((K, H)) / np.sqrt(K) / s, "e2m1")
    wb_words, wb_scales = pack_weight(n((H, N)) / np.sqrt(H) / u * amp, "e4m3")
    return {
        "tab_words": tab_words, "tab_scales": tab_scales,
        "offs": striped(np.random.permutation(T)[:S]),
        "gT": n((H, T)).astype(np.float32),
        "w1_words": w1_words, "w1_scales": w1_scales,
        "b1": (0.5 * n(H)).astype(np.float32),
        "w2": (n((K, H)) / np.sqrt(K) / s * u.T).astype(np.float32),
        "wb_words": wb_words, "wb_scales": wb_scales,
        "ymean": (0.5 * n(N) * amp).astype(np.float32),
    }

def reference(tab_words, tab_scales, offs, gT, w1_words, w1_scales, b1, w2, wb_words, wb_scales, ymean):
    v = unpack_weight(tab_words, tab_scales, "e4m3")[:, unstriped(offs)]
    g = f64(gT)[:, unstriped(offs)]
    w1 = unpack_weight(w1_words, w1_scales, "e2m1")
    wb = unpack_weight(wb_words, wb_scales, "e4m3")
    a = np.tanh((w1.T @ v) + f64(b1)[:, None])
    b = mxq(f64(w2), 0, "e4m3").T @ v
    c = a * b * g
    y = (wb.T @ mxq(c, 0, "e4m3")) + f64(ymean)[:, None]
    words, scales = planes(y)
    return y, words, scales

@@ -1,0 +1,242 @@
+from contextlib import ExitStack
+
+import concourse.mybir as mybir
+
+K, T, S, H, N = 1024, 2048, 1024, 512, 1024
+FLOPS = 2 * (2 * K * H * S + H * N * S)
+
+F32 = mybir.dt.float32
+BF16 = mybir.dt.bfloat16
+I32 = mybir.dt.int32
+U32 = mybir.dt.uint32
+U16 = mybir.dt.uint16
+U8 = mybir.dt.uint8
+FP8X4 = mybir.dt.float8_e4m3fn_x4
+FP4X4 = mybir.dt.float4_e2m1fn_x4
+ACT = mybir.ActivationFunctionType
+MULT = mybir.AluOpType.mult
+
+P = 128
+PACK = 4
+KP = P * PACK
+HALF = 512
+BCOLS = 128
+CHUNK = 256
+SCALAR_WEAVES = 3
+
+
+def tile_list_modal_operator_query_kernel(
+    tc, tab_words, tab_scales, offs, gT, w1_words, w1_scales, b1, w2, wb_words, wb_scales, ymean, out_0, out_1, out_2
+):
+    nc = tc.nc
+    passes = K // KP
+    groups = N // KP
+
+    with ExitStack() as ctx:
+        keep = ctx.enter_context(tc.tile_pool(name="keep", bufs=1))
+        psum = ctx.enter_context(tc.psum_pool(name="psum", bufs=4))
+
+        def sb(shape, dtype, name, after=None):
+            return keep.tile(shape, dtype, name=name, tag=after or name, align_bytes=64)
+
+        offsets = keep.tile([P, S // 16], U16, name="offsets")
+        tab_sc = sb([P, T], U8, "tab_sc")
+        picked_sc = sb([P, S], U8, "picked_sc")
+        v_sc = [sb([P, S], U8, "v_sc%d" % a) for a in range(passes)]
+        w1_sc_raw = sb([P, passes * H], U8, "w1_sc_raw")
+        w1_raw = sb([P, passes * 2 * H], U8, "w1_raw")
+        tab = [sb([P, T], I32, "tab%d" % a) for a in range(passes)]
+        w2_raw = [sb([P, PACK, H], F32, "w2_raw0")]
+        bias1 = sb([P, PACK], F32, "bias1")
+
+        for q in range(4):
+            nc.vector.memset(tab_sc[32 * q : 32 * q + 24, :].bitcast(I32), 0)
+        nc.gpsimd.memset(w1_sc_raw[:].bitcast(I32), 0)
+
+        nc.sync.dma_start(offsets[:], offs)
+        for q in range(4):
+            nc.sync.dma_start(
+                tab_sc[32 * q + 24 : 32 * q + 32, :].bitcast(I32), tab_scales[:, 4 * q : 4 * q + 4, :].bitcast(I32)
+            )
+        nc.sync.dma_start(
+            w1_raw[:].bitcast(I32).rearrange("p (a n) -> p a n", a=passes),
+            w1_words.bitcast(I32).rearrange("a p n -> p a n"),
+        )
+        for a in range(passes):
+            nc.sync.dma_start(tab[a][:], tab_words[a].rearrange("p n i -> p (n i)").bitcast(I32))
+        gT_rows = gT.rearrange("(p t) n -> t p n", t=PACK)
+        w2_rows = w2.rearrange("(a p i) r -> a p i r", a=passes, i=PACK)
+        for q in range(4):
+            nc.sync.dma_start(
+                w1_sc_raw[32 * q : 32 * q + 4, :].bitcast(I32).rearrange("r (a e) -> r a e", a=passes),
+                w1_scales[:, 4 * q : 4 * q + 4, :].bitcast(I32).rearrange("a r e -> r a e"),
+            )
+        nc.sync.dma_start(bias1[:], b1.rearrange("(p t) -> p t", t=PACK))
+        nc.sync.dma_start(w2_raw[0][:], w2_rows[0])
+        for a in range(passes):
+            nc.gpsimd.memset(v_sc[a][96:128, :].bitcast(I32), 0)
+
+        nc.vector.tensor_copy(picked_sc[:], tab_sc[:].indirect(offsets[:]))
+        for a in range(passes):
+            nc.sync.dma_start(v_sc[a][0:100, :].bitcast(I32), picked_sc[24 + 4 * a : 124 + 4 * a, :].bitcast(I32))
+
+        w1_codes = sb([P, passes * 2 * H], U8, "w1_codes")
+        nc.vector.tensor_copy(
+            w1_codes[:].rearrange("p (a t m b) -> p a t m b", a=passes, t=PACK, b=2),
+            w1_raw[:].rearrange("p (a m t b) -> p a t m b", a=passes, t=PACK, b=2),
+        )
+        w1_sc = sb([P, passes * H], U8, "w1_sc")
+        nc.vector.tensor_copy(
+            w1_sc[:].rearrange("p (a t m) -> p a t m", a=passes, t=PACK),
+            w1_sc_raw[:].rearrange("p (a m t) -> p a t m", a=passes, t=PACK),
+        )
+
+        def list_cols(h):
+            return offsets[:, h * HALF // 16 : (h + 1) * HALF // 16]
+
+        v = [[sb([P, HALF], U32, "v%d_%d" % (a, h)) for h in range(2)] for a in range(passes)]
+        resp = [[sb([P, HALF], F32, "resp%d_%d" % (t, h)) for h in range(2)] for t in range(PACK)]
+        for h in range(2):
+            for a in range(passes):
+                nc.vector.tensor_copy(v[a][h][:], tab[a][:].bitcast(U32).indirect(list_cols(h)))
+            for t in range(PACK):
+                acc = psum.tile([P, HALF], F32, name="acc", tag="acc")
+                for a in range(passes):
+                    c0 = a * H + t * P
+                    nc.tensor.matmul_mx(
+                        acc[:],
+                        lhsT=w1_codes[:, 2 * c0 : 2 * (c0 + P)].bitcast(FP4X4),
+                        lhsT_scale=w1_sc[:, c0 : c0 + P],
+                        rhs=v[a][h][:].bitcast(FP8X4),
+                        rhs_scale=v_sc[a][:, h * HALF : (h + 1) * HALF],
+                        start=(a == 0),
+                        stop=(a == passes - 1),
+                    )
+                nc.scalar.activation(resp[t][h][:], acc[:], ACT.Tanh, bias=bias1[:, t : t + 1])
+
+        trunk = [sb([P, T], F32, "trunk0", "tab_sc")]
+        w2_raw.append(sb([P, PACK, H], F32, "w2_raw1", "w1_sc_raw"))
+        trunk.append(sb([P, T], F32, "trunk1", "w1_raw"))
+        trunk.append(sb([P, T], F32, "trunk2", "picked_sc"))
+        wb_sc_raw = sb([P, N], U8, "wb_sc_raw", "tab0")
+        wb_raw = sb([P, N], I32, "wb_raw", "tab1")
+        mean = sb([P, groups, PACK], F32, "mean", "w1_sc")
+        trunk.append(sb([P, T], F32, "trunk3", "w1_codes"))
+        nc.sync.dma_start(trunk[0][:], gT_rows[0])
+        nc.sync.dma_start(trunk[1][:], gT_rows[1])
+        nc.sync.dma_start(w2_raw[1][:], w2_rows[1])
+        nc.sync.dma_start(trunk[2][:], gT_rows[2])
+        nc.gpsimd.memset(wb_sc_raw[:].bitcast(I32), 0)
+        for q in range(4):
+            nc.sync.dma_start(
+                wb_sc_raw[32 * q : 32 * q + 4, :].bitcast(I32), wb_scales[0, 4 * q : 4 * q + 4, :].bitcast(I32)
+            )
+        nc.sync.dma_start(wb_raw[:], wb_words[0].rearrange("p n i -> p (n i)").bitcast(I32))
+        nc.sync.dma_start(trunk[3][:], gT_rows[3])
+        nc.sync.dma_start(mean[:], ymean.rearrange("(g p t) -> p g t", g=groups, t=PACK))
+
+        w2_codes, w2_sc = [], []
+        for a in range(passes):
+            grouped = sb([P, H * PACK], BF16, "w2_bf%d" % a)
+            nc.scalar.copy(
+                grouped[:].rearrange("p (t m i) -> p m i t", t=PACK, i=PACK),
+                w2_raw[a][:].rearrange("p i (m t) -> p m i t", t=PACK),
+            )
+            codes = sb([P, H], U32, "w2_codes%d" % a)
+            sc = sb([P, H], U8, "w2_sc%d" % a)
+            nc.vector.quantize_mx(codes[:].bitcast(FP8X4), sc[:], grouped[:])
+            w2_codes.append(codes)
+            w2_sc.append(sc)
+
+        wb_codes = sb([P, N], I32, "wb_codes")
+        nc.vector.tensor_copy(
+            wb_codes[:].rearrange("p (g t m) -> p g m t", g=groups, t=PACK),
+            wb_raw[:].rearrange("p (g m t) -> p g m t", g=groups, t=PACK),
+        )
+        wb_sc = sb([P, N], U8, "wb_sc")
+        nc.vector.tensor_copy(
+            wb_sc[:].rearrange("p (g t m) -> p g t m", g=groups, t=PACK),
+            wb_sc_raw[:].rearrange("p (g m t) -> p g t m", g=groups, t=PACK),
+        )
+
+        gated = sb([P, PACK + 2, HALF], F32, "gated")
+        y_sc = sb([P, groups * S], U8, "y_sc")
+        for h in range(2):
+            first = 2 * (1 - h)
+            for t in range(PACK - 1):
+                nc.vector.tensor_tensor(gated[:, first + t, :], trunk[t][:].indirect(list_cols(h)), resp[t][h][:], MULT)
+            for u in range(HALF // CHUNK):
+                chunk = h * (HALF // CHUNK) + u
+                nc.vector.tensor_tensor(
+                    gated[:, first + PACK - 1, u * CHUNK : (u + 1) * CHUNK],
+                    trunk[PACK - 1][:].indirect(offsets[:, chunk * CHUNK // 16 : (chunk + 1) * CHUNK // 16]),
+                    resp[PACK - 1][h][:, u * CHUNK : (u + 1) * CHUNK],
+                    MULT,
+                )
+                c_bf = sb([P, CHUNK, PACK], BF16, "c_bf%d" % chunk)
+                for w in range(CHUNK // BCOLS):
+                    j0 = u * CHUNK + w * BCOLS
+                    lin = psum.tile([P, PACK, BCOLS], F32, name="lin", tag="lin")
+                    for t in range(PACK):
+                        for a in range(passes):
+                            nc.tensor.matmul_mx(
+                                lin[:, t, :],
+                                lhsT=w2_codes[a][:, t * P : (t + 1) * P].bitcast(FP8X4),
+                                lhsT_scale=w2_sc[a][:, t * P : (t + 1) * P],
+                                rhs=v[a][h][:, j0 : j0 + BCOLS].bitcast(FP8X4),
+                                rhs_scale=v_sc[a][:, h * HALF + j0 : h * HALF + j0 + BCOLS],
+                                start=(a == 0),
+                                stop=(a == passes - 1),
+                            )
+                    nc.vector.tensor_tensor(
+                        c_bf[:, w * BCOLS : (w + 1) * BCOLS, :].rearrange("p (c i) t -> p c t i", i=4),
+                        lin[:].rearrange("p t (c i) -> p c t i", i=4),
+                        gated[:, first : first + PACK, j0 : j0 + BCOLS].rearrange("p t (c i) -> p c t i", i=4),
+                        MULT,
+                    )
+                c_codes = sb([P, CHUNK], U32, "c_codes%d" % chunk)
+                c_sc = sb([P, CHUNK], U8, "c_sc%d" % chunk)
+                nc.vector.quantize_mx(c_codes[:].bitcast(FP8X4), c_sc[:], c_bf[:].rearrange("p j t -> p (j t)"))
+
+                cols = slice(chunk * CHUNK, (chunk + 1) * CHUNK)
+                for g in range(groups):
+                    y = sb([P, PACK, CHUNK], F32, "y%d_%d" % (chunk, g))
+                    for pair in range(2):
+                        acc = psum.tile([P, 2 * CHUNK], F32, name="acc", tag="acc")
+                        for s in range(2):
+                            n0 = g * KP + (2 * pair + s) * P
+                            nc.tensor.matmul_mx(
+                                acc[:, s * CHUNK : (s + 1) * CHUNK],
+                                lhsT=wb_codes[:, n0 : n0 + P].bitcast(FP8X4),
+                                lhsT_scale=wb_sc[:, n0 : n0 + P],
+                                rhs=c_codes[:].bitcast(FP8X4),
+                                rhs_scale=c_sc[:],
+                                start=True,
+                                stop=True,
+                            )
+                        for s in range(2):
+                            t = 2 * pair + s
+                            nc.scalar.activation(
+                                y[:, t, :], acc[:, s * CHUNK : (s + 1) * CHUNK], ACT.Identity, bias=mean[:, g, t : t + 1]
+                            )
+                    nc.sync.dma_start(out_0[g * KP : (g + 1) * KP, cols].rearrange("(p t) j -> p t j", t=PACK), y[:])
+                    y_bf = sb([P, CHUNK, PACK], BF16, "y_bf%d_%d" % (chunk, g))
+                    woven = y_bf[:].rearrange("p (c i) t -> p c t i", i=4)
+                    rows = y[:].rearrange("p t (c i) -> p c t i", i=4)
+                    if chunk * groups + g < SCALAR_WEAVES:
+                        nc.scalar.copy(woven, rows)
+                    else:
+                        nc.vector.tensor_copy(woven, rows)
+                    y_codes = sb([P, CHUNK], I32, "y_codes%d_%d" % (chunk, g))
+                    nc.vector.quantize_mx(
+                        y_codes[:].bitcast(FP8X4),
+                        y_sc[:, g * S + chunk * CHUNK : g * S + (chunk + 1) * CHUNK],
+                        y_bf[:].rearrange("p j t -> p (j t)"),
+                    )
+                    nc.sync.dma_start(out_1[g].rearrange("p j t -> p (j t)").bitcast(I32)[:, cols], y_codes[:])
+        for q in range(4):
+            queue = nc.sync if q % 2 == 0 else nc.scalar
+            queue.dma_start(
+                out_2[:, 4 * q : 4 * q + 4, :].bitcast(I32).rearrange("g r j -> r g j"),
+                y_sc[32 * q : 32 * q + 4, :].bitcast(I32).rearrange("r (g j) -> r g j", g=groups),
+            )

@@ -23,6 +23,7 @@ HALF = 512
 BCOLS = 128
 CHUNK = 256
 SCALAR_WEAVES = 3
+EARLY = 2
 
 
 def tile_list_modal_operator_query_kernel(
@@ -48,6 +49,7 @@ def tile_list_modal_operator_query_kernel(
         tab = [sb([P, T], I32, "tab%d" % a) for a in range(passes)]
         w2_raw = [sb([P, PACK, H], F32, "w2_raw0")]
         bias1 = sb([P, PACK], F32, "bias1")
+        mean = sb([P, groups, PACK], F32, "mean")
 
         for q in range(4):
             nc.vector.memset(tab_sc[32 * q : 32 * q + 24, :].bitcast(I32), 0)
@@ -73,6 +75,7 @@ def tile_list_modal_operator_query_kernel(
             )
         nc.sync.dma_start(bias1[:], b1.rearrange("(p t) -> p t", t=PACK))
         nc.sync.dma_start(w2_raw[0][:], w2_rows[0])
+        nc.sync.dma_start(mean[:], ymean.rearrange("(g p t) -> p g t", g=groups, t=PACK))
         for a in range(passes):
             nc.gpsimd.memset(v_sc[a][96:128, :].bitcast(I32), 0)
 
@@ -82,8 +85,8 @@ def tile_list_modal_operator_query_kernel(
 
         w1_codes = sb([P, passes * 2 * H], U8, "w1_codes")
         nc.vector.tensor_copy(
-            w1_codes[:].rearrange("p (a t m b) -> p a t m b", a=passes, t=PACK, b=2),
-            w1_raw[:].rearrange("p (a m t b) -> p a t m b", a=passes, t=PACK, b=2),
+            w1_codes[:].bitcast(U16).rearrange("p (a t m) -> p a t m", a=passes, t=PACK),
+            w1_raw[:].bitcast(U16).rearrange("p (a m t) -> p a t m", a=passes, t=PACK),
         )
         w1_sc = sb([P, passes * H], U8, "w1_sc")
         nc.vector.tensor_copy(
@@ -119,9 +122,8 @@ def tile_list_modal_operator_query_kernel(
         trunk.append(sb([P, T], F32, "trunk1", "w1_raw"))
         trunk.append(sb([P, T], F32, "trunk2", "picked_sc"))
         wb_sc_raw = sb([P, N], U8, "wb_sc_raw", "tab0")
-        wb_raw = sb([P, N], I32, "wb_raw", "tab1")
-        mean = sb([P, groups, PACK], F32, "mean", "w1_sc")
-        trunk.append(sb([P, T], F32, "trunk3", "w1_codes"))
+        wb_raw = [sb([P, KP], I32, "wb_raw0", "w1_codes"), sb([P, KP], I32, "wb_raw1", "w1_sc")]
+        trunk.append(sb([P, T], F32, "trunk3", "tab1"))
         nc.sync.dma_start(trunk[0][:], gT_rows[0])
         nc.sync.dma_start(trunk[1][:], gT_rows[1])
         nc.sync.dma_start(w2_raw[1][:], w2_rows[1])
@@ -131,16 +133,17 @@ def tile_list_modal_operator_query_kernel(
             nc.sync.dma_start(
                 wb_sc_raw[32 * q : 32 * q + 4, :].bitcast(I32), wb_scales[0, 4 * q : 4 * q + 4, :].bitcast(I32)
             )
-        nc.sync.dma_start(wb_raw[:], wb_words[0].rearrange("p n i -> p (n i)").bitcast(I32))
         nc.sync.dma_start(trunk[3][:], gT_rows[3])
-        nc.sync.dma_start(mean[:], ymean.rearrange("(g p t) -> p g t", g=groups, t=PACK))
+        wb_cols = wb_words[0].rearrange("p n i -> p (n i)").bitcast(I32)
+        for g in range(groups):
+            nc.sync.dma_start(wb_raw[g][:], wb_cols[:, g * KP : (g + 1) * KP])
 
         w2_codes, w2_sc = [], []
         for a in range(passes):
             grouped = sb([P, H * PACK], BF16, "w2_bf%d" % a)
             nc.scalar.copy(
-                grouped[:].rearrange("p (t m i) -> p m i t", t=PACK, i=PACK),
-                w2_raw[a][:].rearrange("p i (m t) -> p m i t", t=PACK),
+                grouped[:].rearrange("p (t m i) -> p m t i", t=PACK, i=PACK),
+                w2_raw[a][:].rearrange("p i (m t) -> p m t i", t=PACK),
             )
             codes = sb([P, H], U32, "w2_codes%d" % a)
             sc = sb([P, H], U8, "w2_sc%d" % a)
@@ -148,27 +151,17 @@ def tile_list_modal_operator_query_kernel(
             w2_codes.append(codes)
             w2_sc.append(sc)
 
-        wb_codes = sb([P, N], I32, "wb_codes")
-        nc.vector.tensor_copy(
-            wb_codes[:].rearrange("p (g t m) -> p g m t", g=groups, t=PACK),
-            wb_raw[:].rearrange("p (g m t) -> p g m t", g=groups, t=PACK),
-        )
-        wb_sc = sb([P, N], U8, "wb_sc")
-        nc.vector.tensor_copy(
-            wb_sc[:].rearrange("p (g t m) -> p g t m", g=groups, t=PACK),
-            wb_sc_raw[:].rearrange("p (g m t) -> p g t m", g=groups, t=PACK),
-        )
-
-        gated = sb([P, PACK + 2, HALF], F32, "gated")
         y_sc = sb([P, groups * S], U8, "y_sc")
+        gated_rows = sb([P, PACK + EARLY, HALF], F32, "gated_rows")
         for h in range(2):
-            first = 2 * (1 - h)
+            first = (1 - h) * EARLY
+            gated = gated_rows[:, first : first + PACK, :]
             for t in range(PACK - 1):
-                nc.vector.tensor_tensor(gated[:, first + t, :], trunk[t][:].indirect(list_cols(h)), resp[t][h][:], MULT)
+                nc.vector.tensor_tensor(gated[:, t, :], trunk[t][:].indirect(list_cols(h)), resp[t][h][:], MULT)
             for u in range(HALF // CHUNK):
                 chunk = h * (HALF // CHUNK) + u
                 nc.vector.tensor_tensor(
-                    gated[:, first + PACK - 1, u * CHUNK : (u + 1) * CHUNK],
+                    gated[:, PACK - 1, u * CHUNK : (u + 1) * CHUNK],
                     trunk[PACK - 1][:].indirect(offsets[:, chunk * CHUNK // 16 : (chunk + 1) * CHUNK // 16]),
                     resp[PACK - 1][h][:, u * CHUNK : (u + 1) * CHUNK],
                     MULT,
@@ -189,14 +182,27 @@ def tile_list_modal_operator_query_kernel(
                                 stop=(a == passes - 1),
                             )
                     nc.vector.tensor_tensor(
-                        c_bf[:, w * BCOLS : (w + 1) * BCOLS, :].rearrange("p (c i) t -> p c t i", i=4),
-                        lin[:].rearrange("p t (c i) -> p c t i", i=4),
-                        gated[:, first : first + PACK, j0 : j0 + BCOLS].rearrange("p t (c i) -> p c t i", i=4),
+                        c_bf[:, w * BCOLS : (w + 1) * BCOLS, :].rearrange("p (c i) t -> p c t i", i=2),
+                        lin[:].rearrange("p t (c i) -> p c t i", i=2),
+                        gated[:, :, j0 : j0 + BCOLS].rearrange("p t (c i) -> p c t i", i=2),
                         MULT,
                     )
                 c_codes = sb([P, CHUNK], U32, "c_codes%d" % chunk)
                 c_sc = sb([P, CHUNK], U8, "c_sc%d" % chunk)
                 nc.vector.quantize_mx(c_codes[:].bitcast(FP8X4), c_sc[:], c_bf[:].rearrange("p j t -> p (j t)"))
+
+                if chunk == 0:
+                    wb_codes = [sb([P, KP], I32, "wb_codes%d" % g) for g in range(groups)]
+                    for g in range(groups):
+                        nc.vector.tensor_copy(
+                            wb_codes[g][:].rearrange("p (t m i) -> p m t i", t=PACK, i=4),
+                            wb_raw[g][:].rearrange("p (m i t) -> p m t i", t=PACK, i=4),
+                        )
+                    wb_sc = sb([P, N], U8, "wb_sc")
+                    nc.vector.tensor_copy(
+                        wb_sc[:].rearrange("p (g t m) -> p g t m", g=groups, t=PACK),
+                        wb_sc_raw[:].rearrange("p (g m t) -> p g t m", g=groups, t=PACK),
+                    )
 
                 cols = slice(chunk * CHUNK, (chunk + 1) * CHUNK)
                 for g in range(groups):
@@ -207,7 +213,7 @@ def tile_list_modal_operator_query_kernel(
                             n0 = g * KP + (2 * pair + s) * P
                             nc.tensor.matmul_mx(
                                 acc[:, s * CHUNK : (s + 1) * CHUNK],
-                                lhsT=wb_codes[:, n0 : n0 + P].bitcast(FP8X4),
+                                lhsT=wb_codes[g][:, n0 - g * KP : n0 - g * KP + P].bitcast(FP8X4),
                                 lhsT_scale=wb_sc[:, n0 : n0 + P],
                                 rhs=c_codes[:].bitcast(FP8X4),
                                 rhs_scale=c_sc[:],
@@ -221,8 +227,8 @@ def tile_list_modal_operator_query_kernel(
                             )
                     nc.sync.dma_start(out_0[g * KP : (g + 1) * KP, cols].rearrange("(p t) j -> p t j", t=PACK), y[:])
                     y_bf = sb([P, CHUNK, PACK], BF16, "y_bf%d_%d" % (chunk, g))
-                    woven = y_bf[:].rearrange("p (c i) t -> p c t i", i=4)
-                    rows = y[:].rearrange("p t (c i) -> p c t i", i=4)
+                    woven = y_bf[:].rearrange("p (c i) t -> p c t i", i=2)
+                    rows = y[:].rearrange("p t (c i) -> p c t i", i=2)
                     if chunk * groups + g < SCALAR_WEAVES:
                         nc.scalar.copy(woven, rows)
                     else:

@@ -22,8 +22,8 @@ KP = P * PACK
 HALF = 512
 BCOLS = 128
 CHUNK = 256
-SCALAR_WEAVES = 3
-EARLY = 2
+EARLY = 3
+SPANS = ((0, 128), (128, 128), (256, 256), (512, 256), (768, 256))
 
 
 def tile_list_modal_operator_query_kernel(
@@ -44,45 +44,43 @@ def tile_list_modal_operator_query_kernel(
         tab_sc = sb([P, T], U8, "tab_sc")
         picked_sc = sb([P, S], U8, "picked_sc")
         v_sc = [sb([P, S], U8, "v_sc%d" % a) for a in range(passes)]
-        w1_sc_raw = sb([P, passes * H], U8, "w1_sc_raw")
+        sc_raw = sb([P, passes * H], U8, "sc_raw")
         w1_raw = sb([P, passes * 2 * H], U8, "w1_raw")
         tab = [sb([P, T], I32, "tab%d" % a) for a in range(passes)]
-        w2_raw = [sb([P, PACK, H], F32, "w2_raw0")]
         bias1 = sb([P, PACK], F32, "bias1")
-        mean = sb([P, groups, PACK], F32, "mean")
 
-        for q in range(4):
-            nc.vector.memset(tab_sc[32 * q : 32 * q + 24, :].bitcast(I32), 0)
-        nc.gpsimd.memset(w1_sc_raw[:].bitcast(I32), 0)
+        nc.gpsimd.memset(sc_raw[:].bitcast(I32), 0)
+        for first, last in ((0, 16), (32, 48), (64, 128)):
+            nc.vector.memset(tab_sc[first:last, :].bitcast(I32), 0)
 
         nc.sync.dma_start(offsets[:], offs)
-        for q in range(4):
-            nc.sync.dma_start(
-                tab_sc[32 * q + 24 : 32 * q + 32, :].bitcast(I32), tab_scales[:, 4 * q : 4 * q + 4, :].bitcast(I32)
-            )
+        tab_sc_rows = tab_scales.bitcast(I32).rearrange("a (h y r) t -> y (a h) r t", h=2, y=2)
+        for y in range(2):
+            nc.sync.dma_start(tab_sc[32 * y + 16 : 32 * y + 32, :].bitcast(I32), tab_sc_rows[y])
+        nc.sync.dma_start(tab[0][:], tab_words[0].rearrange("p n i -> p (n i)").bitcast(I32))
         nc.sync.dma_start(
             w1_raw[:].bitcast(I32).rearrange("p (a n) -> p a n", a=passes),
             w1_words.bitcast(I32).rearrange("a p n -> p a n"),
         )
-        for a in range(passes):
-            nc.sync.dma_start(tab[a][:], tab_words[a].rearrange("p n i -> p (n i)").bitcast(I32))
-        gT_rows = gT.rearrange("(p t) n -> t p n", t=PACK)
-        w2_rows = w2.rearrange("(a p i) r -> a p i r", a=passes, i=PACK)
+        nc.sync.dma_start(bias1[:], b1.rearrange("(p t) -> p t", t=PACK))
         for q in range(4):
             nc.sync.dma_start(
-                w1_sc_raw[32 * q : 32 * q + 4, :].bitcast(I32).rearrange("r (a e) -> r a e", a=passes),
+                sc_raw[32 * q : 32 * q + 4, :].bitcast(I32).rearrange("r (a e) -> r a e", a=passes),
                 w1_scales[:, 4 * q : 4 * q + 4, :].bitcast(I32).rearrange("a r e -> r a e"),
             )
-        nc.sync.dma_start(bias1[:], b1.rearrange("(p t) -> p t", t=PACK))
-        nc.sync.dma_start(w2_raw[0][:], w2_rows[0])
-        nc.sync.dma_start(mean[:], ymean.rearrange("(g p t) -> p g t", g=groups, t=PACK))
-        for a in range(passes):
-            nc.gpsimd.memset(v_sc[a][96:128, :].bitcast(I32), 0)
+        nc.sync.dma_start(tab[1][:], tab_words[1].rearrange("p n i -> p (n i)").bitcast(I32))
 
         nc.vector.tensor_copy(picked_sc[:], tab_sc[:].indirect(offsets[:]))
         for a in range(passes):
-            nc.sync.dma_start(v_sc[a][0:100, :].bitcast(I32), picked_sc[24 + 4 * a : 124 + 4 * a, :].bitcast(I32))
+            for h in range(2):
+                row = 16 + 4 * (2 * a + h)
+                nc.sync.dma_start(v_sc[a][64 * h : 64 * h + 64, :].bitcast(I32), picked_sc[row : row + 64, :].bitcast(I32))
 
+        def list_cols(first, count):
+            return offsets[:, first // 16 : (first + count) // 16]
+
+        v = [[sb([P, HALF], U32, "v%d_%d" % (a, h)) for h in range(2)] for a in range(passes)]
+        nc.vector.tensor_copy(v[0][0][:], tab[0][:].bitcast(U32).indirect(list_cols(0, HALF)))
         w1_codes = sb([P, passes * 2 * H], U8, "w1_codes")
         nc.vector.tensor_copy(
             w1_codes[:].bitcast(U16).rearrange("p (a t m) -> p a t m", a=passes, t=PACK),
@@ -91,17 +89,14 @@ def tile_list_modal_operator_query_kernel(
         w1_sc = sb([P, passes * H], U8, "w1_sc")
         nc.vector.tensor_copy(
             w1_sc[:].rearrange("p (a t m) -> p a t m", a=passes, t=PACK),
-            w1_sc_raw[:].rearrange("p (a m t) -> p a t m", a=passes, t=PACK),
+            sc_raw[:].rearrange("p (a m t) -> p a t m", a=passes, t=PACK),
         )
+        nc.vector.tensor_copy(v[1][0][:], tab[1][:].bitcast(U32).indirect(list_cols(0, HALF)))
+        for a in range(passes):
+            nc.vector.tensor_copy(v[a][1][:], tab[a][:].bitcast(U32).indirect(list_cols(HALF, HALF)))
 
-        def list_cols(h):
-            return offsets[:, h * HALF // 16 : (h + 1) * HALF // 16]
-
-        v = [[sb([P, HALF], U32, "v%d_%d" % (a, h)) for h in range(2)] for a in range(passes)]
         resp = [[sb([P, HALF], F32, "resp%d_%d" % (t, h)) for h in range(2)] for t in range(PACK)]
         for h in range(2):
-            for a in range(passes):
-                nc.vector.tensor_copy(v[a][h][:], tab[a][:].bitcast(U32).indirect(list_cols(h)))
             for t in range(PACK):
                 acc = psum.tile([P, HALF], F32, name="acc", tag="acc")
                 for a in range(passes):
@@ -117,129 +112,169 @@ def tile_list_modal_operator_query_kernel(
                     )
                 nc.scalar.activation(resp[t][h][:], acc[:], ACT.Tanh, bias=bias1[:, t : t + 1])
 
-        trunk = [sb([P, T], F32, "trunk0", "tab_sc")]
-        w2_raw.append(sb([P, PACK, H], F32, "w2_raw1", "w1_sc_raw"))
-        trunk.append(sb([P, T], F32, "trunk1", "w1_raw"))
-        trunk.append(sb([P, T], F32, "trunk2", "picked_sc"))
-        wb_sc_raw = sb([P, N], U8, "wb_sc_raw", "tab0")
-        wb_raw = [sb([P, KP], I32, "wb_raw0", "w1_codes"), sb([P, KP], I32, "wb_raw1", "w1_sc")]
-        trunk.append(sb([P, T], F32, "trunk3", "tab1"))
+        gT_rows = gT.rearrange("(p t) n -> t p n", t=PACK)
+        w2_rows = w2.rearrange("(a p i) r -> a p i r", a=passes, i=PACK)
+        trunk = [
+            sb([P, T], F32, "trunk%d" % t, after)
+            for t, after in enumerate(("tab_sc", "w1_raw", "tab1", "w1_sc"))
+        ]
+        w2_raw = sb([P, PACK, H], F32, "w2_raw0", "tab0")
+        w2_late = [
+            sb([P, PACK, H // 2], F32, "w2_late%d" % u, after) for u, after in enumerate(("picked_sc", "w1_codes"))
+        ]
+        wb_raw = sb([P, N], I32, "wb_raw", "bias1")
+        mean = sb([P, groups, PACK], F32, "mean", "tab_sc")
         nc.sync.dma_start(trunk[0][:], gT_rows[0])
         nc.sync.dma_start(trunk[1][:], gT_rows[1])
-        nc.sync.dma_start(w2_raw[1][:], w2_rows[1])
-        nc.sync.dma_start(trunk[2][:], gT_rows[2])
-        nc.gpsimd.memset(wb_sc_raw[:].bitcast(I32), 0)
         for q in range(4):
             nc.sync.dma_start(
-                wb_sc_raw[32 * q : 32 * q + 4, :].bitcast(I32), wb_scales[0, 4 * q : 4 * q + 4, :].bitcast(I32)
+                sc_raw[32 * q : 32 * q + 8, :KP].bitcast(I32),
+                wb_scales[0, 4 * q : 4 * q + 4, :].bitcast(I32).rearrange("r (g e) -> g r e", g=groups),
             )
+        nc.sync.dma_start(w2_raw[:], w2_rows[0])
+        nc.sync.dma_start(w2_late[0][:], w2_rows[1][:, :, : H // 2])
+        nc.sync.dma_start(trunk[2][:], gT_rows[2])
+        nc.sync.dma_start(w2_late[1][:], w2_rows[1][:, :, H // 2 :])
+        nc.sync.dma_start(mean[:], ymean.rearrange("(g p t) -> p g t", g=groups, t=PACK))
         nc.sync.dma_start(trunk[3][:], gT_rows[3])
         wb_cols = wb_words[0].rearrange("p n i -> p (n i)").bitcast(I32)
         for g in range(groups):
-            nc.sync.dma_start(wb_raw[g][:], wb_cols[:, g * KP : (g + 1) * KP])
+            nc.sync.dma_start(wb_raw[:, g * KP : (g + 1) * KP], wb_cols[:, g * KP : (g + 1) * KP])
+
+        gated_rows = sb([P, PACK + EARLY, HALF], F32, "gated_rows")
+        gated = [gated_rows[:, EARLY:, :], gated_rows[:, :PACK, :]]
+
+        def gate(t, first, count):
+            h, j0 = divmod(first, HALF)
+            nc.vector.tensor_tensor(
+                gated[h][:, t, j0 : j0 + count],
+                trunk[t][:].indirect(list_cols(first, count)),
+                resp[t][h][:, j0 : j0 + count],
+                MULT,
+            )
+
+        for t in range(PACK - 1):
+            gate(t, 0, HALF)
+            if t < EARLY:
+                gate(t, HALF, HALF)
+        wb_sc = sb([P, KP], U8, "wb_sc")
+        nc.vector.tensor_copy(
+            wb_sc[:].rearrange("p (t m) -> p t m", t=PACK),
+            sc_raw[:, :KP].rearrange("p (m t) -> p t m", t=PACK),
+        )
 
         w2_codes, w2_sc = [], []
         for a in range(passes):
             grouped = sb([P, H * PACK], BF16, "w2_bf%d" % a)
-            nc.scalar.copy(
-                grouped[:].rearrange("p (t m i) -> p m t i", t=PACK, i=PACK),
-                w2_raw[a][:].rearrange("p i (m t) -> p m t i", t=PACK),
-            )
+            dealt = grouped[:].rearrange("p (s e m i) -> p m s i e", s=2, e=2, i=PACK)
+            sources = [w2_raw] if a == 0 else w2_late
+            width = P // len(sources)
+            for u, raw in enumerate(sources):
+                nc.scalar.copy(
+                    dealt[:, u * width : (u + 1) * width], raw[:].rearrange("p i (m s e) -> p m s i e", s=2, e=2)
+                )
             codes = sb([P, H], U32, "w2_codes%d" % a)
             sc = sb([P, H], U8, "w2_sc%d" % a)
             nc.vector.quantize_mx(codes[:].bitcast(FP8X4), sc[:], grouped[:])
             w2_codes.append(codes)
             w2_sc.append(sc)
 
-        y_sc = sb([P, groups * S], U8, "y_sc")
-        gated_rows = sb([P, PACK + EARLY, HALF], F32, "gated_rows")
-        for h in range(2):
-            first = (1 - h) * EARLY
-            gated = gated_rows[:, first : first + PACK, :]
-            for t in range(PACK - 1):
-                nc.vector.tensor_tensor(gated[:, t, :], trunk[t][:].indirect(list_cols(h)), resp[t][h][:], MULT)
-            for u in range(HALF // CHUNK):
-                chunk = h * (HALF // CHUNK) + u
+        c_codes, c_sc = [], []
+        wb_codes = [sb([P, KP], I32, "wb_codes%d" % g) for g in range(groups)]
+        for chunk, (first, width) in enumerate(SPANS):
+            h = first // HALF
+            gate(PACK - 1, first, width)
+            c_bf = sb([P, width, PACK], BF16, "c_bf%d" % chunk)
+            for w in range(width // BCOLS):
+                j0 = first % HALF + w * BCOLS
+                lin = psum.tile([P, PACK, BCOLS], F32, name="lin", tag="lin")
+                for a in range(passes):
+                    for t in range(PACK):
+                        nc.tensor.matmul_mx(
+                            lin[:, t, :],
+                            lhsT=w2_codes[a][:, t * P : (t + 1) * P].bitcast(FP8X4),
+                            lhsT_scale=w2_sc[a][:, t * P : (t + 1) * P],
+                            rhs=v[a][h][:, j0 : j0 + BCOLS].bitcast(FP8X4),
+                            rhs_scale=v_sc[a][:, h * HALF + j0 : h * HALF + j0 + BCOLS],
+                            start=(a == 0 and t == 0),
+                            stop=(a == passes - 1 and t == PACK - 1),
+                        )
                 nc.vector.tensor_tensor(
-                    gated[:, PACK - 1, u * CHUNK : (u + 1) * CHUNK],
-                    trunk[PACK - 1][:].indirect(offsets[:, chunk * CHUNK // 16 : (chunk + 1) * CHUNK // 16]),
-                    resp[PACK - 1][h][:, u * CHUNK : (u + 1) * CHUNK],
+                    c_bf[:, w * BCOLS : (w + 1) * BCOLS, :].rearrange("p (c i) t -> p c t i", i=2),
+                    lin[:].rearrange("p t (c i) -> p c t i", i=2),
+                    gated[h][:, :, j0 : j0 + BCOLS].rearrange("p t (c i) -> p c t i", i=2),
                     MULT,
                 )
-                c_bf = sb([P, CHUNK, PACK], BF16, "c_bf%d" % chunk)
-                for w in range(CHUNK // BCOLS):
-                    j0 = u * CHUNK + w * BCOLS
-                    lin = psum.tile([P, PACK, BCOLS], F32, name="lin", tag="lin")
-                    for t in range(PACK):
-                        for a in range(passes):
-                            nc.tensor.matmul_mx(
-                                lin[:, t, :],
-                                lhsT=w2_codes[a][:, t * P : (t + 1) * P].bitcast(FP8X4),
-                                lhsT_scale=w2_sc[a][:, t * P : (t + 1) * P],
-                                rhs=v[a][h][:, j0 : j0 + BCOLS].bitcast(FP8X4),
-                                rhs_scale=v_sc[a][:, h * HALF + j0 : h * HALF + j0 + BCOLS],
-                                start=(a == 0),
-                                stop=(a == passes - 1),
-                            )
-                    nc.vector.tensor_tensor(
-                        c_bf[:, w * BCOLS : (w + 1) * BCOLS, :].rearrange("p (c i) t -> p c t i", i=2),
-                        lin[:].rearrange("p t (c i) -> p c t i", i=2),
-                        gated[:, :, j0 : j0 + BCOLS].rearrange("p t (c i) -> p c t i", i=2),
-                        MULT,
-                    )
-                c_codes = sb([P, CHUNK], U32, "c_codes%d" % chunk)
-                c_sc = sb([P, CHUNK], U8, "c_sc%d" % chunk)
-                nc.vector.quantize_mx(c_codes[:].bitcast(FP8X4), c_sc[:], c_bf[:].rearrange("p j t -> p (j t)"))
-
-                if chunk == 0:
-                    wb_codes = [sb([P, KP], I32, "wb_codes%d" % g) for g in range(groups)]
-                    for g in range(groups):
-                        nc.vector.tensor_copy(
-                            wb_codes[g][:].rearrange("p (t m i) -> p m t i", t=PACK, i=4),
-                            wb_raw[g][:].rearrange("p (m i t) -> p m t i", t=PACK, i=4),
-                        )
-                    wb_sc = sb([P, N], U8, "wb_sc")
-                    nc.vector.tensor_copy(
-                        wb_sc[:].rearrange("p (g t m) -> p g t m", g=groups, t=PACK),
-                        wb_sc_raw[:].rearrange("p (g m t) -> p g t m", g=groups, t=PACK),
-                    )
-
-                cols = slice(chunk * CHUNK, (chunk + 1) * CHUNK)
+            c_codes.append(sb([P, width], U32, "c_codes%d" % chunk))
+            c_sc.append(sb([P, width], U8, "c_sc%d" % chunk))
+            nc.vector.quantize_mx(
+                c_codes[chunk][:].bitcast(FP8X4), c_sc[chunk][:], c_bf[:].rearrange("p j t -> p (j t)")
+            )
+            if chunk == 0:
                 for g in range(groups):
-                    y = sb([P, PACK, CHUNK], F32, "y%d_%d" % (chunk, g))
-                    for pair in range(2):
-                        acc = psum.tile([P, 2 * CHUNK], F32, name="acc", tag="acc")
-                        for s in range(2):
-                            n0 = g * KP + (2 * pair + s) * P
-                            nc.tensor.matmul_mx(
-                                acc[:, s * CHUNK : (s + 1) * CHUNK],
-                                lhsT=wb_codes[g][:, n0 - g * KP : n0 - g * KP + P].bitcast(FP8X4),
-                                lhsT_scale=wb_sc[:, n0 : n0 + P],
-                                rhs=c_codes[:].bitcast(FP8X4),
-                                rhs_scale=c_sc[:],
-                                start=True,
-                                stop=True,
-                            )
-                        for s in range(2):
-                            t = 2 * pair + s
-                            nc.scalar.activation(
-                                y[:, t, :], acc[:, s * CHUNK : (s + 1) * CHUNK], ACT.Identity, bias=mean[:, g, t : t + 1]
-                            )
-                    nc.sync.dma_start(out_0[g * KP : (g + 1) * KP, cols].rearrange("(p t) j -> p t j", t=PACK), y[:])
-                    y_bf = sb([P, CHUNK, PACK], BF16, "y_bf%d_%d" % (chunk, g))
-                    woven = y_bf[:].rearrange("p (c i) t -> p c t i", i=2)
-                    rows = y[:].rearrange("p t (c i) -> p c t i", i=2)
-                    if chunk * groups + g < SCALAR_WEAVES:
-                        nc.scalar.copy(woven, rows)
-                    else:
-                        nc.vector.tensor_copy(woven, rows)
-                    y_codes = sb([P, CHUNK], I32, "y_codes%d_%d" % (chunk, g))
-                    nc.vector.quantize_mx(
-                        y_codes[:].bitcast(FP8X4),
-                        y_sc[:, g * S + chunk * CHUNK : g * S + (chunk + 1) * CHUNK],
-                        y_bf[:].rearrange("p j t -> p (j t)"),
+                    nc.vector.tensor_copy(
+                        wb_codes[g][:].rearrange("p (t m i) -> p m t i", t=PACK, i=4),
+                        wb_raw[:, g * KP : (g + 1) * KP].rearrange("p (m i t) -> p m t i", t=PACK, i=4),
                     )
-                    nc.sync.dma_start(out_1[g].rearrange("p j t -> p (j t)").bitcast(I32)[:, cols], y_codes[:])
+
+        y = [[sb([P, PACK, HALF], F32, "y%d_%d" % (h, g)) for g in range(groups)] for h in range(2)]
+
+        def weave(copy, g, first, width, after=None):
+            h, j0 = divmod(first, HALF)
+            y_bf = sb([P, width, PACK], BF16, "y_bf%d_%d" % (first, g), after)
+            copy(
+                y_bf[:].rearrange("p (c i) t -> p c t i", i=2),
+                y[h][g][:, :, j0 : j0 + width].rearrange("p t (c i) -> p c t i", i=2),
+            )
+            return y_bf
+
+        for chunk, (first, width) in enumerate(SPANS):
+            h, j0 = divmod(first, HALF)
+            per_bank = HALF // width
+            for g in range(groups):
+                for t0 in range(0, PACK, per_bank):
+                    acc = psum.tile([P, per_bank, width], F32, name="acc", tag="acc")
+                    for s in range(per_bank):
+                        m0 = (t0 + s) * P
+                        nc.tensor.matmul_mx(
+                            acc[:, s, :],
+                            lhsT=wb_codes[g][:, m0 : m0 + P].bitcast(FP8X4),
+                            lhsT_scale=wb_sc[4 * g :, m0 : m0 + P],
+                            rhs=c_codes[chunk][:].bitcast(FP8X4),
+                            rhs_scale=c_sc[chunk][:],
+                            start=True,
+                            stop=True,
+                        )
+                    for s in range(per_bank):
+                        t = t0 + s
+                        nc.scalar.activation(
+                            y[h][g][:, t, j0 : j0 + width], acc[:, s, :], ACT.Identity, bias=mean[:, g, t : t + 1]
+                        )
+                nc.sync.dma_start(
+                    out_0[g * KP : (g + 1) * KP, first : first + width].rearrange("(p t) j -> p t j", t=PACK),
+                    y[h][g][:, :, j0 : j0 + width],
+                )
+
+        y_sc = sb([P, groups * S], U8, "y_sc")
+
+        def planes(y_bf, g, first, width, after=None):
+            y_codes = sb([P, width], I32, "y_codes%d_%d" % (first, g), after)
+            nc.vector.quantize_mx(
+                y_codes[:].bitcast(FP8X4),
+                y_sc[:, g * S + first : g * S + first + width],
+                y_bf[:].rearrange("p j t -> p (j t)"),
+            )
+            nc.sync.dma_start(
+                out_1[g].rearrange("p j t -> p (j t)").bitcast(I32)[:, first : first + width], y_codes[:]
+            )
+
+        vec, act = nc.vector.tensor_copy, nc.scalar.copy
+        for g in range(groups):
+            planes(weave(vec, g, 0, HALF, ("gated_rows", "c_bf4")[g]), g, 0, HALF, ("c_codes4", "c_sc4")[g])
+        for g in range(groups):
+            planes(weave(vec, g, HALF, CHUNK), g, HALF, CHUNK, ("wb_codes1", "wb_sc")[g])
+        for g in range(groups):
+            planes(weave(act, g, HALF + CHUNK, CHUNK), g, HALF + CHUNK, CHUNK)
         for q in range(4):
             queue = nc.sync if q % 2 == 0 else nc.scalar
             queue.dma_start(

@@ -23,7 +23,7 @@ HALF = 512
 BCOLS = 128
 CHUNK = 256
 EARLY = 3
-SPANS = ((0, 128), (128, 128), (256, 256), (512, 256), (768, 256))
+SPANS = ((0, 256), (256, 256), (512, 256), (768, 256))
 
 
 def tile_list_modal_operator_query_kernel(
@@ -219,6 +219,8 @@ def tile_list_modal_operator_query_kernel(
 
         y = [[sb([P, PACK, HALF], F32, "y%d_%d" % (h, g)) for g in range(groups)] for h in range(2)]
 
+        first_bf = []
+
         def weave(copy, g, first, width, after=None):
             h, j0 = divmod(first, HALF)
             y_bf = sb([P, width, PACK], BF16, "y_bf%d_%d" % (first, g), after)
@@ -230,6 +232,8 @@ def tile_list_modal_operator_query_kernel(
 
         for chunk, (first, width) in enumerate(SPANS):
             h, j0 = divmod(first, HALF)
+            if first >= HALF:
+                first_bf.append(weave(nc.scalar.copy, len(first_bf), 0, CHUNK))
             per_bank = HALF // width
             for g in range(groups):
                 for t0 in range(0, PACK, per_bank):
@@ -270,9 +274,11 @@ def tile_list_modal_operator_query_kernel(
 
         vec, act = nc.vector.tensor_copy, nc.scalar.copy
         for g in range(groups):
-            planes(weave(vec, g, 0, HALF, ("gated_rows", "c_bf4")[g]), g, 0, HALF, ("c_codes4", "c_sc4")[g])
+            planes(weave(vec, g, CHUNK, CHUNK, ("gated_rows", "c_bf3")[g]), g, CHUNK, CHUNK)
         for g in range(groups):
-            planes(weave(vec, g, HALF, CHUNK), g, HALF, CHUNK, ("wb_codes1", "wb_sc")[g])
+            planes(first_bf[g], g, 0, CHUNK)
+        for g in range(groups):
+            planes(weave(vec, g, HALF, CHUNK), g, HALF, CHUNK)
         for g in range(groups):
             planes(weave(act, g, HALF + CHUNK, CHUNK), g, HALF + CHUNK, CHUNK)
         for q in range(4):

@@ -23,7 +23,7 @@ HALF = 512
 BCOLS = 128
 CHUNK = 256
 EARLY = 3
-SPANS = ((0, 256), (256, 256), (512, 256), (768, 256))
+SPANS = ((0, 128), (128, 128), (256, 256), (512, 256), (768, 256))
 
 
 def tile_list_modal_operator_query_kernel(
@@ -219,8 +219,6 @@ def tile_list_modal_operator_query_kernel(
 
         y = [[sb([P, PACK, HALF], F32, "y%d_%d" % (h, g)) for g in range(groups)] for h in range(2)]
 
-        first_bf = []
-
         def weave(copy, g, first, width, after=None):
             h, j0 = divmod(first, HALF)
             y_bf = sb([P, width, PACK], BF16, "y_bf%d_%d" % (first, g), after)
@@ -232,8 +230,6 @@ def tile_list_modal_operator_query_kernel(
 
         for chunk, (first, width) in enumerate(SPANS):
             h, j0 = divmod(first, HALF)
-            if first >= HALF:
-                first_bf.append(weave(nc.scalar.copy, len(first_bf), 0, CHUNK))
             per_bank = HALF // width
             for g in range(groups):
                 for t0 in range(0, PACK, per_bank):
@@ -254,7 +250,7 @@ def tile_list_modal_operator_query_kernel(
                         nc.scalar.activation(
                             y[h][g][:, t, j0 : j0 + width], acc[:, s, :], ACT.Identity, bias=mean[:, g, t : t + 1]
                         )
-                nc.sync.dma_start(
+                nc.scalar.dma_start(
                     out_0[g * KP : (g + 1) * KP, first : first + width].rearrange("(p t) j -> p t j", t=PACK),
                     y[h][g][:, :, j0 : j0 + width],
                 )
@@ -274,9 +270,7 @@ def tile_list_modal_operator_query_kernel(
 
         vec, act = nc.vector.tensor_copy, nc.scalar.copy
         for g in range(groups):
-            planes(weave(vec, g, CHUNK, CHUNK, ("gated_rows", "c_bf3")[g]), g, CHUNK, CHUNK)
-        for g in range(groups):
-            planes(first_bf[g], g, 0, CHUNK)
+            planes(weave(vec, g, 0, HALF, ("c_codes3", "c_bf4")[g]), g, 0, HALF)
         for g in range(groups):
             planes(weave(vec, g, HALF, CHUNK), g, HALF, CHUNK)
         for g in range(groups):

@@ -271,10 +271,25 @@ def tile_list_modal_operator_query_kernel(
         vec, act = nc.vector.tensor_copy, nc.scalar.copy
         for g in range(groups):
             planes(weave(vec, g, 0, HALF, ("c_codes3", "c_bf4")[g]), g, 0, HALF)
+        both = sb([P, groups, CHUNK], I32, "y_codes_both")
         for g in range(groups):
-            planes(weave(vec, g, HALF, CHUNK), g, HALF, CHUNK)
-        for g in range(groups):
-            planes(weave(act, g, HALF + CHUNK, CHUNK), g, HALF + CHUNK, CHUNK)
+            nc.vector.quantize_mx(
+                both[:, g, :].bitcast(FP8X4),
+                y_sc[:, g * S + HALF : g * S + HALF + CHUNK],
+                weave(vec, g, HALF, CHUNK)[:].rearrange("p j t -> p (j t)"),
+            )
+        nc.sync.dma_start(
+            out_1.rearrange("g p j t -> p g (j t)").bitcast(I32)[:, :, HALF : HALF + CHUNK], both[:]
+        )
+        last = HALF + CHUNK
+        shared = sb([P, CHUNK, PACK], BF16, "y_bf_last")
+        for copy, j0 in ((act, 0), (vec, CHUNK // 2)):
+            copy(
+                shared[:, j0 : j0 + CHUNK // 2, :].rearrange("p (c i) t -> p c t i", i=2),
+                y[1][0][:, :, CHUNK + j0 : CHUNK + j0 + CHUNK // 2].rearrange("p t (c i) -> p c t i", i=2),
+            )
+        planes(shared, 0, last, CHUNK)
+        planes(weave(act, 1, last, CHUNK), 1, last, CHUNK)
         for q in range(4):
             queue = nc.sync if q % 2 == 0 else nc.scalar
             queue.dma_start(

@@ -19,11 +19,12 @@ MULT = mybir.AluOpType.mult
 P = 128
 PACK = 4
 KP = P * PACK
-HALF = 512
-BCOLS = 128
+QUADS = 4
+BANK = 512
+HALF = S // 2
+BLOCK = BANK // PACK
 CHUNK = 256
-EARLY = 3
-SPANS = ((0, 128), (128, 128), (256, 256), (512, 256), (768, 256))
+SPANS = ((0, BLOCK), (BLOCK, BLOCK), (CHUNK, CHUNK), (2 * CHUNK, CHUNK), (3 * CHUNK, CHUNK))
 
 
 def tile_list_modal_operator_query_kernel(
@@ -50,20 +51,20 @@ def tile_list_modal_operator_query_kernel(
         bias1 = sb([P, PACK], F32, "bias1")
 
         nc.gpsimd.memset(sc_raw[:].bitcast(I32), 0)
-        for first, last in ((0, 16), (32, 48), (64, 128)):
-            nc.vector.memset(tab_sc[first:last, :].bitcast(I32), 0)
+        for row0, row1 in ((0, 16), (32, 48), (64, P)):
+            nc.vector.memset(tab_sc[row0:row1, :].bitcast(I32), 0)
 
         nc.sync.dma_start(offsets[:], offs)
-        tab_sc_rows = tab_scales.bitcast(I32).rearrange("a (h y r) t -> y (a h) r t", h=2, y=2)
-        for y in range(2):
-            nc.sync.dma_start(tab_sc[32 * y + 16 : 32 * y + 32, :].bitcast(I32), tab_sc_rows[y])
+        tab_sc_rows = tab_scales.bitcast(I32).rearrange("a (u o r) t -> o (a u) r t", u=2, o=2)
+        for odd in range(2):
+            nc.sync.dma_start(tab_sc[32 * odd + 16 : 32 * odd + 32, :].bitcast(I32), tab_sc_rows[odd])
         nc.sync.dma_start(tab[0][:], tab_words[0].rearrange("p n i -> p (n i)").bitcast(I32))
         nc.sync.dma_start(
             w1_raw[:].bitcast(I32).rearrange("p (a n) -> p a n", a=passes),
             w1_words.bitcast(I32).rearrange("a p n -> p a n"),
         )
         nc.sync.dma_start(bias1[:], b1.rearrange("(p t) -> p t", t=PACK))
-        for q in range(4):
+        for q in range(QUADS):
             nc.sync.dma_start(
                 sc_raw[32 * q : 32 * q + 4, :].bitcast(I32).rearrange("r (a e) -> r a e", a=passes),
                 w1_scales[:, 4 * q : 4 * q + 4, :].bitcast(I32).rearrange("a r e -> r a e"),
@@ -72,9 +73,11 @@ def tile_list_modal_operator_query_kernel(
 
         nc.vector.tensor_copy(picked_sc[:], tab_sc[:].indirect(offsets[:]))
         for a in range(passes):
-            for h in range(2):
-                row = 16 + 4 * (2 * a + h)
-                nc.sync.dma_start(v_sc[a][64 * h : 64 * h + 64, :].bitcast(I32), picked_sc[row : row + 64, :].bitcast(I32))
+            for upper in range(2):
+                row = 16 + 4 * (2 * a + upper)
+                nc.sync.dma_start(
+                    v_sc[a][64 * upper : 64 * upper + 64, :].bitcast(I32), picked_sc[row : row + 64, :].bitcast(I32)
+                )
 
         def list_cols(first, count):
             return offsets[:, first // 16 : (first + count) // 16]
@@ -100,63 +103,61 @@ def tile_list_modal_operator_query_kernel(
             for t in range(PACK):
                 acc = psum.tile([P, HALF], F32, name="acc", tag="acc")
                 for a in range(passes):
-                    c0 = a * H + t * P
+                    col = a * H + t * P
                     nc.tensor.matmul_mx(
                         acc[:],
-                        lhsT=w1_codes[:, 2 * c0 : 2 * (c0 + P)].bitcast(FP4X4),
-                        lhsT_scale=w1_sc[:, c0 : c0 + P],
+                        lhsT=w1_codes[:, 2 * col : 2 * (col + P)].bitcast(FP4X4),
+                        lhsT_scale=w1_sc[:, col : col + P],
                         rhs=v[a][h][:].bitcast(FP8X4),
                         rhs_scale=v_sc[a][:, h * HALF : (h + 1) * HALF],
                         start=(a == 0),
                         stop=(a == passes - 1),
                     )
-                nc.scalar.activation(resp[t][h][:], acc[:], ACT.Tanh, bias=bias1[:, t : t + 1])
+                now = HALF
+                if (h, t) == (0, PACK - 1):
+                    held, now = acc, CHUNK
+                nc.scalar.activation(resp[t][h][:, :now], acc[:, :now], ACT.Tanh, bias=bias1[:, t : t + 1])
 
         gT_rows = gT.rearrange("(p t) n -> t p n", t=PACK)
         w2_rows = w2.rearrange("(a p i) r -> a p i r", a=passes, i=PACK)
         trunk = [
-            sb([P, T], F32, "trunk%d" % t, after)
-            for t, after in enumerate(("tab_sc", "w1_raw", "tab1", "w1_sc"))
+            sb([P, T], F32, "trunk%d" % t, after) for t, after in enumerate(("tab_sc", "w1_raw", "tab1", "w1_sc"))
         ]
-        w2_raw = sb([P, PACK, H], F32, "w2_raw0", "tab0")
-        w2_late = [
-            sb([P, PACK, H // 2], F32, "w2_late%d" % u, after) for u, after in enumerate(("picked_sc", "w1_codes"))
+        w2_first = sb([P, PACK, H], F32, "w2_first", "tab0")
+        w2_second = [
+            sb([P, PACK, H // 2], F32, "w2_second%d" % u, after) for u, after in enumerate(("picked_sc", "w1_codes"))
         ]
-        wb_raw = sb([P, N], I32, "wb_raw", "bias1")
+        wb_raw = [sb([P, KP], I32, "wb_raw%d" % g, "resp0_%d" % g) for g in range(groups)]
         mean = sb([P, groups, PACK], F32, "mean", "tab_sc")
         nc.sync.dma_start(trunk[0][:], gT_rows[0])
         nc.sync.dma_start(trunk[1][:], gT_rows[1])
-        for q in range(4):
+        for q in range(QUADS):
             nc.sync.dma_start(
                 sc_raw[32 * q : 32 * q + 8, :KP].bitcast(I32),
                 wb_scales[0, 4 * q : 4 * q + 4, :].bitcast(I32).rearrange("r (g e) -> g r e", g=groups),
             )
-        nc.sync.dma_start(w2_raw[:], w2_rows[0])
-        nc.sync.dma_start(w2_late[0][:], w2_rows[1][:, :, : H // 2])
+        nc.sync.dma_start(w2_first[:], w2_rows[0])
+        nc.sync.dma_start(w2_second[0][:], w2_rows[1][:, :, : H // 2])
         nc.sync.dma_start(trunk[2][:], gT_rows[2])
-        nc.sync.dma_start(w2_late[1][:], w2_rows[1][:, :, H // 2 :])
+        nc.sync.dma_start(w2_second[1][:], w2_rows[1][:, :, H // 2 :])
         nc.sync.dma_start(mean[:], ymean.rearrange("(g p t) -> p g t", g=groups, t=PACK))
         nc.sync.dma_start(trunk[3][:], gT_rows[3])
         wb_cols = wb_words[0].rearrange("p n i -> p (n i)").bitcast(I32)
         for g in range(groups):
-            nc.sync.dma_start(wb_raw[:, g * KP : (g + 1) * KP], wb_cols[:, g * KP : (g + 1) * KP])
+            nc.sync.dma_start(wb_raw[g][:], wb_cols[:, g * KP : (g + 1) * KP])
 
-        gated_rows = sb([P, PACK + EARLY, HALF], F32, "gated_rows")
-        gated = [gated_rows[:, EARLY:, :], gated_rows[:, :PACK, :]]
+        gated_rows = sb([P, 2 * PACK - 1, HALF], F32, "gated_rows")
+        gated = [gated_rows[:, PACK - 1 :, :], gated_rows[:, :PACK, :]]
 
-        def gate(t, first, count):
+        def gate(t, first, count, response):
             h, j0 = divmod(first, HALF)
             nc.vector.tensor_tensor(
-                gated[h][:, t, j0 : j0 + count],
-                trunk[t][:].indirect(list_cols(first, count)),
-                resp[t][h][:, j0 : j0 + count],
-                MULT,
+                gated[h][:, t, j0 : j0 + count], trunk[t][:].indirect(list_cols(first, count)), response, MULT
             )
 
         for t in range(PACK - 1):
-            gate(t, 0, HALF)
-            if t < EARLY:
-                gate(t, HALF, HALF)
+            for h in range(2):
+                gate(t, h * HALF, HALF, resp[t][h][:])
         wb_sc = sb([P, KP], U8, "wb_sc")
         nc.vector.tensor_copy(
             wb_sc[:].rearrange("p (t m) -> p t m", t=PACK),
@@ -164,45 +165,48 @@ def tile_list_modal_operator_query_kernel(
         )
 
         w2_codes, w2_sc = [], []
-        for a in range(passes):
+        for a, sources in enumerate(([w2_first], w2_second)):
             grouped = sb([P, H * PACK], BF16, "w2_bf%d" % a)
             dealt = grouped[:].rearrange("p (s e m i) -> p m s i e", s=2, e=2, i=PACK)
-            sources = [w2_raw] if a == 0 else w2_late
-            width = P // len(sources)
+            share = P // len(sources)
             for u, raw in enumerate(sources):
                 nc.scalar.copy(
-                    dealt[:, u * width : (u + 1) * width], raw[:].rearrange("p i (m s e) -> p m s i e", s=2, e=2)
+                    dealt[:, u * share : (u + 1) * share], raw[:].rearrange("p i (m s e) -> p m s i e", s=2, e=2)
                 )
-            codes = sb([P, H], U32, "w2_codes%d" % a)
-            sc = sb([P, H], U8, "w2_sc%d" % a)
-            nc.vector.quantize_mx(codes[:].bitcast(FP8X4), sc[:], grouped[:])
-            w2_codes.append(codes)
-            w2_sc.append(sc)
+            w2_codes.append(sb([P, H], U32, "w2_codes%d" % a))
+            w2_sc.append(sb([P, H], U8, "w2_sc%d" % a))
+            nc.vector.quantize_mx(w2_codes[a][:].bitcast(FP8X4), w2_sc[a][:], grouped[:])
 
         c_codes, c_sc = [], []
         wb_codes = [sb([P, KP], I32, "wb_codes%d" % g) for g in range(groups)]
         for chunk, (first, width) in enumerate(SPANS):
             h = first // HALF
-            gate(PACK - 1, first, width)
+            if first == CHUNK:
+                late = sb([P, CHUNK], F32, "resp_late", "resp0_0")
+                nc.scalar.activation(late[:], held[:, CHUNK:], ACT.Tanh, bias=bias1[:, PACK - 1 :])
+                response = late[:]
+            else:
+                response = resp[PACK - 1][h][:, first % HALF : first % HALF + width]
+            gate(PACK - 1, first, width, response)
             c_bf = sb([P, width, PACK], BF16, "c_bf%d" % chunk)
-            for w in range(width // BCOLS):
-                j0 = first % HALF + w * BCOLS
-                lin = psum.tile([P, PACK, BCOLS], F32, name="lin", tag="lin")
+            for w in range(width // BLOCK):
+                j0 = first % HALF + w * BLOCK
+                lin = psum.tile([P, PACK, BLOCK], F32, name="lin", tag="lin")
                 for a in range(passes):
                     for t in range(PACK):
                         nc.tensor.matmul_mx(
                             lin[:, t, :],
                             lhsT=w2_codes[a][:, t * P : (t + 1) * P].bitcast(FP8X4),
                             lhsT_scale=w2_sc[a][:, t * P : (t + 1) * P],
-                            rhs=v[a][h][:, j0 : j0 + BCOLS].bitcast(FP8X4),
-                            rhs_scale=v_sc[a][:, h * HALF + j0 : h * HALF + j0 + BCOLS],
+                            rhs=v[a][h][:, j0 : j0 + BLOCK].bitcast(FP8X4),
+                            rhs_scale=v_sc[a][:, h * HALF + j0 : h * HALF + j0 + BLOCK],
                             start=(a == 0 and t == 0),
                             stop=(a == passes - 1 and t == PACK - 1),
                         )
                 nc.vector.tensor_tensor(
-                    c_bf[:, w * BCOLS : (w + 1) * BCOLS, :].rearrange("p (c i) t -> p c t i", i=2),
+                    c_bf[:, w * BLOCK : (w + 1) * BLOCK, :].rearrange("p (c i) t -> p c t i", i=2),
                     lin[:].rearrange("p t (c i) -> p c t i", i=2),
-                    gated[h][:, :, j0 : j0 + BCOLS].rearrange("p t (c i) -> p c t i", i=2),
+                    gated[h][:, :, j0 : j0 + BLOCK].rearrange("p t (c i) -> p c t i", i=2),
                     MULT,
                 )
             c_codes.append(sb([P, width], U32, "c_codes%d" % chunk))
@@ -214,32 +218,22 @@ def tile_list_modal_operator_query_kernel(
                 for g in range(groups):
                     nc.vector.tensor_copy(
                         wb_codes[g][:].rearrange("p (t m i) -> p m t i", t=PACK, i=4),
-                        wb_raw[:, g * KP : (g + 1) * KP].rearrange("p (m i t) -> p m t i", t=PACK, i=4),
+                        wb_raw[g][:].rearrange("p (m i t) -> p m t i", t=PACK, i=4),
                     )
 
         y = [[sb([P, PACK, HALF], F32, "y%d_%d" % (h, g)) for g in range(groups)] for h in range(2)]
-
-        def weave(copy, g, first, width, after=None):
-            h, j0 = divmod(first, HALF)
-            y_bf = sb([P, width, PACK], BF16, "y_bf%d_%d" % (first, g), after)
-            copy(
-                y_bf[:].rearrange("p (c i) t -> p c t i", i=2),
-                y[h][g][:, :, j0 : j0 + width].rearrange("p t (c i) -> p c t i", i=2),
-            )
-            return y_bf
-
         for chunk, (first, width) in enumerate(SPANS):
             h, j0 = divmod(first, HALF)
-            per_bank = HALF // width
+            per_bank = BANK // width
             for g in range(groups):
                 for t0 in range(0, PACK, per_bank):
                     acc = psum.tile([P, per_bank, width], F32, name="acc", tag="acc")
                     for s in range(per_bank):
-                        m0 = (t0 + s) * P
+                        col = (t0 + s) * P
                         nc.tensor.matmul_mx(
                             acc[:, s, :],
-                            lhsT=wb_codes[g][:, m0 : m0 + P].bitcast(FP8X4),
-                            lhsT_scale=wb_sc[4 * g :, m0 : m0 + P],
+                            lhsT=wb_codes[g][:, col : col + P].bitcast(FP8X4),
+                            lhsT_scale=wb_sc[4 * g :, col : col + P],
                             rhs=c_codes[chunk][:].bitcast(FP8X4),
                             rhs_scale=c_sc[chunk][:],
                             start=True,
@@ -250,47 +244,51 @@ def tile_list_modal_operator_query_kernel(
                         nc.scalar.activation(
                             y[h][g][:, t, j0 : j0 + width], acc[:, s, :], ACT.Identity, bias=mean[:, g, t : t + 1]
                         )
-                nc.scalar.dma_start(
+                queue = nc.sync if h == 0 else nc.scalar
+                queue.dma_start(
                     out_0[g * KP : (g + 1) * KP, first : first + width].rearrange("(p t) j -> p t j", t=PACK),
                     y[h][g][:, :, j0 : j0 + width],
                 )
 
         y_sc = sb([P, groups * S], U8, "y_sc")
+        words_out = out_1.rearrange("g p j t -> p g (j t)").bitcast(I32)
 
-        def planes(y_bf, g, first, width, after=None):
-            y_codes = sb([P, width], I32, "y_codes%d_%d" % (first, g), after)
+        def weave(shares, g, first, after=None):
+            h, j0 = divmod(first, HALF)
+            y_bf = sb([P, sum(count for copy, count in shares), PACK], BF16, "y_bf%d_%d" % (first, g), after)
+            done = 0
+            for copy, count in shares:
+                copy(
+                    y_bf[:, done : done + count, :].rearrange("p (c i) t -> p c t i", i=2),
+                    y[h][g][:, :, j0 + done : j0 + done + count].rearrange("p t (c i) -> p c t i", i=2),
+                )
+                done += count
+            return y_bf
+
+        def quantise(codes, y_bf, g, first, width):
             nc.vector.quantize_mx(
-                y_codes[:].bitcast(FP8X4),
+                codes.bitcast(FP8X4),
                 y_sc[:, g * S + first : g * S + first + width],
                 y_bf[:].rearrange("p j t -> p (j t)"),
             )
-            nc.sync.dma_start(
-                out_1[g].rearrange("p j t -> p (j t)").bitcast(I32)[:, first : first + width], y_codes[:]
-            )
+
+        def planes(y_bf, g, first, width):
+            y_codes = sb([P, width], I32, "y_codes%d_%d" % (first, g))
+            quantise(y_codes[:], y_bf, g, first, width)
+            nc.sync.dma_start(words_out[:, g, first : first + width], y_codes[:])
 
         vec, act = nc.vector.tensor_copy, nc.scalar.copy
-        for g in range(groups):
-            planes(weave(vec, g, 0, HALF, ("c_codes3", "c_bf4")[g]), g, 0, HALF)
+        last_chunk = len(SPANS) - 1
+        for g, after in enumerate(("c_codes%d" % (last_chunk - 1), "c_bf%d" % last_chunk)):
+            planes(weave([(vec, HALF)], g, 0, after), g, 0, HALF)
         both = sb([P, groups, CHUNK], I32, "y_codes_both")
         for g in range(groups):
-            nc.vector.quantize_mx(
-                both[:, g, :].bitcast(FP8X4),
-                y_sc[:, g * S + HALF : g * S + HALF + CHUNK],
-                weave(vec, g, HALF, CHUNK)[:].rearrange("p j t -> p (j t)"),
-            )
-        nc.sync.dma_start(
-            out_1.rearrange("g p j t -> p g (j t)").bitcast(I32)[:, :, HALF : HALF + CHUNK], both[:]
-        )
-        last = HALF + CHUNK
-        shared = sb([P, CHUNK, PACK], BF16, "y_bf_last")
-        for copy, j0 in ((act, 0), (vec, CHUNK // 2)):
-            copy(
-                shared[:, j0 : j0 + CHUNK // 2, :].rearrange("p (c i) t -> p c t i", i=2),
-                y[1][0][:, :, CHUNK + j0 : CHUNK + j0 + CHUNK // 2].rearrange("p t (c i) -> p c t i", i=2),
-            )
-        planes(shared, 0, last, CHUNK)
-        planes(weave(act, 1, last, CHUNK), 1, last, CHUNK)
-        for q in range(4):
+            quantise(both[:, g, :], weave([(vec, CHUNK)], g, HALF), g, HALF, CHUNK)
+        nc.sync.dma_start(words_out[:, :, HALF : HALF + CHUNK], both[:])
+        first = S - CHUNK
+        for g, shares in enumerate(([(act, CHUNK // 2), (vec, CHUNK // 2)], [(act, CHUNK)])):
+            planes(weave(shares, g, first), g, first, CHUNK)
+        for q in range(QUADS):
             queue = nc.sync if q % 2 == 0 else nc.scalar
             queue.dma_start(
                 out_2[:, 4 * q : 4 * q + 4, :].bitcast(I32).rearrange("g r j -> r g j"),

@@ -222,33 +222,33 @@ def tile_list_modal_operator_query_kernel(
                     )
 
         y = [[sb([P, PACK, HALF], F32, "y%d_%d" % (h, g)) for g in range(groups)] for h in range(2)]
-        for chunk, (first, width) in enumerate(SPANS):
+
+        def product(chunk, g, t0, first, width):
             h, j0 = divmod(first, HALF)
+            c0 = first - SPANS[chunk][0]
             per_bank = BANK // width
-            for g in range(groups):
-                for t0 in range(0, PACK, per_bank):
-                    acc = psum.tile([P, per_bank, width], F32, name="acc", tag="acc")
-                    for s in range(per_bank):
-                        col = (t0 + s) * P
-                        nc.tensor.matmul_mx(
-                            acc[:, s, :],
-                            lhsT=wb_codes[g][:, col : col + P].bitcast(FP8X4),
-                            lhsT_scale=wb_sc[4 * g :, col : col + P],
-                            rhs=c_codes[chunk][:].bitcast(FP8X4),
-                            rhs_scale=c_sc[chunk][:],
-                            start=True,
-                            stop=True,
-                        )
-                    for s in range(per_bank):
-                        t = t0 + s
-                        nc.scalar.activation(
-                            y[h][g][:, t, j0 : j0 + width], acc[:, s, :], ACT.Identity, bias=mean[:, g, t : t + 1]
-                        )
-                queue = nc.sync if h == 0 else nc.scalar
-                queue.dma_start(
-                    out_0[g * KP : (g + 1) * KP, first : first + width].rearrange("(p t) j -> p t j", t=PACK),
-                    y[h][g][:, :, j0 : j0 + width],
+            acc = psum.tile([P, per_bank, width], F32, name="acc", tag="acc")
+            for s in range(per_bank):
+                col = (t0 + s) * P
+                nc.tensor.matmul_mx(
+                    acc[:, s, :],
+                    lhsT=wb_codes[g][:, col : col + P].bitcast(FP8X4),
+                    lhsT_scale=wb_sc[4 * g :, col : col + P],
+                    rhs=c_codes[chunk][:, c0 : c0 + width].bitcast(FP8X4),
+                    rhs_scale=c_sc[chunk][:, c0 : c0 + width],
+                    start=True,
+                    stop=True,
                 )
+            for s in range(per_bank):
+                t = t0 + s
+                nc.scalar.activation(
+                    y[h][g][:, t, j0 : j0 + width], acc[:, s, :], ACT.Identity, bias=mean[:, g, t : t + 1]
+                )
+
+        def store(queue, g, t0, t1, first, width):
+            h, j0 = divmod(first, HALF)
+            rows = out_0[g * KP : (g + 1) * KP, first : first + width].rearrange("(p t) j -> p t j", t=PACK)
+            queue.dma_start(rows[:, t0:t1, :], y[h][g][:, t0:t1, j0 : j0 + width])
 
         y_sc = sb([P, groups * S], U8, "y_sc")
         words_out = out_1.rearrange("g p j t -> p g (j t)").bitcast(I32)
@@ -272,22 +272,38 @@ def tile_list_modal_operator_query_kernel(
                 y_bf[:].rearrange("p j t -> p (j t)"),
             )
 
-        def planes(y_bf, g, first, width):
-            y_codes = sb([P, width], I32, "y_codes%d_%d" % (first, g))
-            quantise(y_codes[:], y_bf, g, first, width)
-            nc.sync.dma_start(words_out[:, g, first : first + width], y_codes[:])
-
         vec, act = nc.vector.tensor_copy, nc.scalar.copy
-        last_chunk = len(SPANS) - 1
-        for g, after in enumerate(("c_codes%d" % (last_chunk - 1), "c_bf%d" % last_chunk)):
-            planes(weave([(vec, HALF)], g, 0, after), g, 0, HALF)
-        both = sb([P, groups, CHUNK], I32, "y_codes_both")
+        for chunk, (first, width) in enumerate(SPANS[:3]):
+            if chunk == 2:
+                early = weave([(act, CHUNK)], 0, 0)
+            for g in range(groups):
+                for t0 in range(0, PACK, BANK // width):
+                    product(chunk, g, t0, first, width)
+                store(nc.sync, g, 0, PACK, first, width)
         for g in range(groups):
-            quantise(both[:, g, :], weave([(vec, CHUNK)], g, HALF), g, HALF, CHUNK)
-        nc.sync.dma_start(words_out[:, :, HALF : HALF + CHUNK], both[:])
-        first = S - CHUNK
-        for g, shares in enumerate(([(act, CHUNK // 2), (vec, CHUNK // 2)], [(act, CHUNK)])):
-            planes(weave(shares, g, first), g, first, CHUNK)
+            for chunk in (3, 4):
+                for t0 in (0, 2):
+                    product(chunk, g, t0, SPANS[chunk][0], CHUNK)
+                    if chunk == 4:
+                        store(nc.scalar, g, t0, t0 + 2, HALF, HALF)
+
+        y_codes = [
+            [sb([P, HALF], I32, "y_codes%d_%d" % (h, g), "w1_sc" if h + g == 0 else None) for g in range(groups)]
+            for h in range(2)
+        ]
+        rest = weave([(vec, CHUNK)], 0, CHUNK, "c_bf4")
+        quantise(y_codes[0][0][:, CHUNK:], rest, 0, CHUNK, CHUNK)
+        quantise(y_codes[0][0][:, :CHUNK], early, 0, 0, CHUNK)
+        nc.sync.dma_start(words_out[:, 0, :HALF], y_codes[0][0][:])
+        quantise(y_codes[0][1][:], weave([(vec, HALF)], 1, 0, "gated_rows"), 1, 0, HALF)
+        nc.sync.dma_start(words_out[:, 1, :HALF], y_codes[0][1][:])
+        quantise(y_codes[1][0][:], weave([(vec, HALF)], 0, HALF), 0, HALF, HALF)
+        nc.sync.dma_start(words_out[:, 0, HALF:], y_codes[1][0][:])
+        fourth = weave([(vec, CHUNK)], 1, HALF)
+        fifth = weave([(act, CHUNK)], 1, HALF + CHUNK)
+        quantise(y_codes[1][1][:, :CHUNK], fourth, 1, HALF, CHUNK)
+        quantise(y_codes[1][1][:, CHUNK:], fifth, 1, HALF + CHUNK, CHUNK)
+        nc.sync.dma_start(words_out[:, 1, HALF:], y_codes[1][1][:])
         for q in range(QUADS):
             queue = nc.sync if q % 2 == 0 else nc.scalar
             queue.dma_start(

@@ -54,6 +54,14 @@ def tile_list_modal_operator_query_kernel(
         for row0, row1 in ((0, 16), (32, 48), (64, P)):
             nc.vector.memset(tab_sc[row0:row1, :].bitcast(I32), 0)
 
+        wb_sc_raw = sb([P, KP], U8, "wb_sc_raw")
+        nc.gpsimd.memset(wb_sc_raw[:].bitcast(I32), 0)
+        for q in range(QUADS):
+            nc.gpsimd.dma_start(
+                wb_sc_raw[32 * q : 32 * q + 8, :].bitcast(I32),
+                wb_scales[0, 4 * q : 4 * q + 4, :].bitcast(I32).rearrange("r (g e) -> g r e", g=groups),
+            )
+
         nc.sync.dma_start(offsets[:], offs)
         tab_sc_rows = tab_scales.bitcast(I32).rearrange("a (u o r) t -> o (a u) r t", u=2, o=2)
         for odd in range(2):
@@ -128,23 +136,18 @@ def tile_list_modal_operator_query_kernel(
             sb([P, PACK, H // 2], F32, "w2_second%d" % u, after) for u, after in enumerate(("picked_sc", "w1_codes"))
         ]
         wb_raw = [sb([P, KP], I32, "wb_raw%d" % g, "resp0_%d" % g) for g in range(groups)]
-        mean = sb([P, groups, PACK], F32, "mean", "tab_sc")
+        mean = sb([P, groups, PACK], F32, "mean", "resp1_1")
         nc.sync.dma_start(trunk[0][:], gT_rows[0])
         nc.sync.dma_start(trunk[1][:], gT_rows[1])
-        for q in range(QUADS):
-            nc.sync.dma_start(
-                sc_raw[32 * q : 32 * q + 8, :KP].bitcast(I32),
-                wb_scales[0, 4 * q : 4 * q + 4, :].bitcast(I32).rearrange("r (g e) -> g r e", g=groups),
-            )
         nc.sync.dma_start(w2_first[:], w2_rows[0])
         nc.sync.dma_start(w2_second[0][:], w2_rows[1][:, :, : H // 2])
         nc.sync.dma_start(trunk[2][:], gT_rows[2])
         nc.sync.dma_start(w2_second[1][:], w2_rows[1][:, :, H // 2 :])
-        nc.sync.dma_start(mean[:], ymean.rearrange("(g p t) -> p g t", g=groups, t=PACK))
         nc.sync.dma_start(trunk[3][:], gT_rows[3])
         wb_cols = wb_words[0].rearrange("p n i -> p (n i)").bitcast(I32)
         for g in range(groups):
             nc.sync.dma_start(wb_raw[g][:], wb_cols[:, g * KP : (g + 1) * KP])
+        nc.sync.dma_start(mean[:], ymean.rearrange("(g p t) -> p g t", g=groups, t=PACK))
 
         gated_rows = sb([P, 2 * PACK - 1, HALF], F32, "gated_rows")
         gated = [gated_rows[:, PACK - 1 :, :], gated_rows[:, :PACK, :]]
@@ -158,10 +161,10 @@ def tile_list_modal_operator_query_kernel(
         for t in range(PACK - 1):
             for h in range(2):
                 gate(t, h * HALF, HALF, resp[t][h][:])
-        wb_sc = sb([P, KP], U8, "wb_sc")
+        wb_sc = sb([P, KP], U8, "wb_sc", "resp1_0")
         nc.vector.tensor_copy(
             wb_sc[:].rearrange("p (t m) -> p t m", t=PACK),
-            sc_raw[:, :KP].rearrange("p (m t) -> p t m", t=PACK),
+            wb_sc_raw[:].rearrange("p (m t) -> p t m", t=PACK),
         )
 
         w2_codes, w2_sc = [], []
@@ -223,9 +226,9 @@ def tile_list_modal_operator_query_kernel(
 
         y = [[sb([P, PACK, HALF], F32, "y%d_%d" % (h, g)) for g in range(groups)] for h in range(2)]
 
-        def product(chunk, g, t0, first, width):
+        def y_bank(chunk, g, t0):
+            first, width = SPANS[chunk]
             h, j0 = divmod(first, HALF)
-            c0 = first - SPANS[chunk][0]
             per_bank = BANK // width
             acc = psum.tile([P, per_bank, width], F32, name="acc", tag="acc")
             for s in range(per_bank):
@@ -234,8 +237,8 @@ def tile_list_modal_operator_query_kernel(
                     acc[:, s, :],
                     lhsT=wb_codes[g][:, col : col + P].bitcast(FP8X4),
                     lhsT_scale=wb_sc[4 * g :, col : col + P],
-                    rhs=c_codes[chunk][:, c0 : c0 + width].bitcast(FP8X4),
-                    rhs_scale=c_sc[chunk][:, c0 : c0 + width],
+                    rhs=c_codes[chunk][:].bitcast(FP8X4),
+                    rhs_scale=c_sc[chunk][:],
                     start=True,
                     stop=True,
                 )
@@ -253,16 +256,13 @@ def tile_list_modal_operator_query_kernel(
         y_sc = sb([P, groups * S], U8, "y_sc")
         words_out = out_1.rearrange("g p j t -> p g (j t)").bitcast(I32)
 
-        def weave(shares, g, first, after=None):
+        def weave(engine_copy, g, first, width, after=None):
             h, j0 = divmod(first, HALF)
-            y_bf = sb([P, sum(count for copy, count in shares), PACK], BF16, "y_bf%d_%d" % (first, g), after)
-            done = 0
-            for copy, count in shares:
-                copy(
-                    y_bf[:, done : done + count, :].rearrange("p (c i) t -> p c t i", i=2),
-                    y[h][g][:, :, j0 + done : j0 + done + count].rearrange("p t (c i) -> p c t i", i=2),
-                )
-                done += count
+            y_bf = sb([P, width, PACK], BF16, "y_bf%d_%d" % (first, g), after)
+            engine_copy(
+                y_bf[:].rearrange("p (c i) t -> p c t i", i=2),
+                y[h][g][:, :, j0 : j0 + width].rearrange("p t (c i) -> p c t i", i=2),
+            )
             return y_bf
 
         def quantise(codes, y_bf, g, first, width):
@@ -272,37 +272,39 @@ def tile_list_modal_operator_query_kernel(
                 y_bf[:].rearrange("p j t -> p (j t)"),
             )
 
-        vec, act = nc.vector.tensor_copy, nc.scalar.copy
+        on_vector, on_scalar = nc.vector.tensor_copy, nc.scalar.copy
         for chunk, (first, width) in enumerate(SPANS[:3]):
-            if chunk == 2:
-                early = weave([(act, CHUNK)], 0, 0)
+            if first == CHUNK:
+                early = weave(on_scalar, 0, 0, CHUNK)
             for g in range(groups):
                 for t0 in range(0, PACK, BANK // width):
-                    product(chunk, g, t0, first, width)
+                    y_bank(chunk, g, t0)
                 store(nc.sync, g, 0, PACK, first, width)
+        last_chunk = len(SPANS) - 1
         for g in range(groups):
-            for chunk in (3, 4):
-                for t0 in (0, 2):
-                    product(chunk, g, t0, SPANS[chunk][0], CHUNK)
-                    if chunk == 4:
-                        store(nc.scalar, g, t0, t0 + 2, HALF, HALF)
+            for chunk in (last_chunk - 1, last_chunk):
+                for t0 in range(0, PACK, BANK // CHUNK):
+                    y_bank(chunk, g, t0)
+                    if chunk == last_chunk:
+                        store(nc.scalar, g, t0, t0 + BANK // CHUNK, HALF, HALF)
 
         y_codes = [
             [sb([P, HALF], I32, "y_codes%d_%d" % (h, g), "w1_sc" if h + g == 0 else None) for g in range(groups)]
             for h in range(2)
         ]
-        rest = weave([(vec, CHUNK)], 0, CHUNK, "c_bf4")
+        rest = weave(on_vector, 0, CHUNK, CHUNK, "c_bf%d" % last_chunk)
         quantise(y_codes[0][0][:, CHUNK:], rest, 0, CHUNK, CHUNK)
         quantise(y_codes[0][0][:, :CHUNK], early, 0, 0, CHUNK)
         nc.sync.dma_start(words_out[:, 0, :HALF], y_codes[0][0][:])
-        quantise(y_codes[0][1][:], weave([(vec, HALF)], 1, 0, "gated_rows"), 1, 0, HALF)
+        quantise(y_codes[0][1][:], weave(on_vector, 1, 0, HALF, "gated_rows"), 1, 0, HALF)
         nc.sync.dma_start(words_out[:, 1, :HALF], y_codes[0][1][:])
-        quantise(y_codes[1][0][:], weave([(vec, HALF)], 0, HALF), 0, HALF, HALF)
+        quantise(y_codes[1][0][:], weave(on_vector, 0, HALF, HALF), 0, HALF, HALF)
         nc.sync.dma_start(words_out[:, 0, HALF:], y_codes[1][0][:])
-        fourth = weave([(vec, CHUNK)], 1, HALF)
-        fifth = weave([(act, CHUNK)], 1, HALF + CHUNK)
-        quantise(y_codes[1][1][:, :CHUNK], fourth, 1, HALF, CHUNK)
-        quantise(y_codes[1][1][:, CHUNK:], fifth, 1, HALF + CHUNK, CHUNK)
+        tail = [
+            weave(engine_copy, 1, HALF + u * CHUNK, CHUNK) for u, engine_copy in enumerate((on_vector, on_scalar))
+        ]
+        for u, y_bf in enumerate(tail):
+            quantise(y_codes[1][1][:, u * CHUNK : (u + 1) * CHUNK], y_bf, 1, HALF + u * CHUNK, CHUNK)
         nc.sync.dma_start(words_out[:, 1, HALF:], y_codes[1][1][:])
         for q in range(QUADS):
             queue = nc.sync if q % 2 == 0 else nc.scalar

@@ -80,7 +80,7 @@ def tile_list_modal_operator_query_kernel(
         nc.sync.dma_start(tab[1][:], tab_words[1].rearrange("p n i -> p (n i)").bitcast(I32))
 
         nc.vector.tensor_copy(picked_sc[:], tab_sc[:].indirect(offsets[:]))
-        for a in range(passes):
+        for a in reversed(range(passes)):
             for upper in range(2):
                 row = 16 + 4 * (2 * a + upper)
                 nc.sync.dma_start(
@@ -106,25 +106,26 @@ def tile_list_modal_operator_query_kernel(
         for a in range(passes):
             nc.vector.tensor_copy(v[a][1][:], tab[a][:].bitcast(U32).indirect(list_cols(HALF, HALF)))
 
-        resp = [[sb([P, HALF], F32, "resp%d_%d" % (t, h)) for h in range(2)] for t in range(PACK)]
-        for h in range(2):
-            for t in range(PACK):
-                acc = psum.tile([P, HALF], F32, name="acc", tag="acc")
-                for a in range(passes):
-                    col = a * H + t * P
-                    nc.tensor.matmul_mx(
-                        acc[:],
-                        lhsT=w1_codes[:, 2 * col : 2 * (col + P)].bitcast(FP4X4),
-                        lhsT_scale=w1_sc[:, col : col + P],
-                        rhs=v[a][h][:].bitcast(FP8X4),
-                        rhs_scale=v_sc[a][:, h * HALF : (h + 1) * HALF],
-                        start=(a == 0),
-                        stop=(a == passes - 1),
-                    )
-                now = HALF
-                if (h, t) == (0, PACK - 1):
-                    held, now = acc, CHUNK
-                nc.scalar.activation(resp[t][h][:, :now], acc[:, :now], ACT.Tanh, bias=bias1[:, t : t + 1])
+        resp = [[sb([P, HALF], F32, "resp%d_%d" % (t, h)) for h in range(2)] for t in range(PACK - 1)]
+        held = []
+        in_order = [(h, t) for h in range(2) for t in range(2)] + [(h, t) for t in (2, 3) for h in range(2)]
+        for h, t in in_order:
+            acc = psum.tile([P, HALF], F32, name="acc", tag="acc")
+            for a in range(passes):
+                col = a * H + t * P
+                nc.tensor.matmul_mx(
+                    acc[:],
+                    lhsT=w1_codes[:, 2 * col : 2 * (col + P)].bitcast(FP4X4),
+                    lhsT_scale=w1_sc[:, col : col + P],
+                    rhs=v[a][h][:].bitcast(FP8X4),
+                    rhs_scale=v_sc[a][:, h * HALF : (h + 1) * HALF],
+                    start=(a == 0),
+                    stop=(a == passes - 1),
+                )
+            if t == PACK - 1:
+                held.append(acc)
+            else:
+                nc.scalar.activation(resp[t][h][:], acc[:], ACT.Tanh, bias=bias1[:, t : t + 1])
 
         gT_rows = gT.rearrange("(p t) n -> t p n", t=PACK)
         w2_rows = w2.rearrange("(a p i) r -> a p i r", a=passes, i=PACK)
@@ -158,9 +159,8 @@ def tile_list_modal_operator_query_kernel(
                 gated[h][:, t, j0 : j0 + count], trunk[t][:].indirect(list_cols(first, count)), response, MULT
             )
 
-        for t in range(PACK - 1):
-            for h in range(2):
-                gate(t, h * HALF, HALF, resp[t][h][:])
+        for h, t in in_order[:-2]:
+            gate(t, h * HALF, HALF, resp[t][h][:])
         wb_sc = sb([P, KP], U8, "wb_sc", "resp1_0")
         nc.vector.tensor_copy(
             wb_sc[:].rearrange("p (t m) -> p t m", t=PACK),
@@ -180,16 +180,20 @@ def tile_list_modal_operator_query_kernel(
             w2_sc.append(sb([P, H], U8, "w2_sc%d" % a))
             nc.vector.quantize_mx(w2_codes[a][:].bitcast(FP8X4), w2_sc[a][:], grouped[:])
 
+        last_resp = sb([P, 2, HALF], F32, "last_resp", "w1_codes")
+        for h, count in enumerate((CHUNK, HALF)):
+            nc.scalar.activation(last_resp[:, h, :count], held[h][:, :count], ACT.Tanh, bias=bias1[:, PACK - 1 :])
+
         c_codes, c_sc = [], []
         wb_codes = [sb([P, KP], I32, "wb_codes%d" % g) for g in range(groups)]
         for chunk, (first, width) in enumerate(SPANS):
             h = first // HALF
             if first == CHUNK:
                 late = sb([P, CHUNK], F32, "resp_late", "resp0_0")
-                nc.scalar.activation(late[:], held[:, CHUNK:], ACT.Tanh, bias=bias1[:, PACK - 1 :])
+                nc.scalar.activation(late[:], held[0][:, CHUNK:], ACT.Tanh, bias=bias1[:, PACK - 1 :])
                 response = late[:]
             else:
-                response = resp[PACK - 1][h][:, first % HALF : first % HALF + width]
+                response = last_resp[:, h, first % HALF : first % HALF + width]
             gate(PACK - 1, first, width, response)
             c_bf = sb([P, width, PACK], BF16, "c_bf%d" % chunk)
             for w in range(width // BLOCK):
@@ -207,9 +211,9 @@ def tile_list_modal_operator_query_kernel(
                             stop=(a == passes - 1 and t == PACK - 1),
                         )
                 nc.vector.tensor_tensor(
-                    c_bf[:, w * BLOCK : (w + 1) * BLOCK, :].rearrange("p (c i) t -> p c t i", i=2),
-                    lin[:].rearrange("p t (c i) -> p c t i", i=2),
-                    gated[h][:, :, j0 : j0 + BLOCK].rearrange("p t (c i) -> p c t i", i=2),
+                    c_bf[:, w * BLOCK : (w + 1) * BLOCK, :].rearrange("p (c i) t -> p c t i", i=4),
+                    lin[:].rearrange("p t (c i) -> p c t i", i=4),
+                    gated[h][:, :, j0 : j0 + BLOCK].rearrange("p t (c i) -> p c t i", i=4),
                     MULT,
                 )
             c_codes.append(sb([P, width], U32, "c_codes%d" % chunk))
@@ -260,8 +264,8 @@ def tile_list_modal_operator_query_kernel(
             h, j0 = divmod(first, HALF)
             y_bf = sb([P, width, PACK], BF16, "y_bf%d_%d" % (first, g), after)
             engine_copy(
-                y_bf[:].rearrange("p (c i) t -> p c t i", i=2),
-                y[h][g][:, :, j0 : j0 + width].rearrange("p t (c i) -> p c t i", i=2),
+                y_bf[:].rearrange("p (c i) t -> p c t i", i=4),
+                y[h][g][:, :, j0 : j0 + width].rearrange("p t (c i) -> p c t i", i=4),
             )
             return y_bf
 
@@ -304,8 +308,10 @@ def tile_list_modal_operator_query_kernel(
             weave(engine_copy, 1, HALF + u * CHUNK, CHUNK) for u, engine_copy in enumerate((on_vector, on_scalar))
         ]
         for u, y_bf in enumerate(tail):
-            quantise(y_codes[1][1][:, u * CHUNK : (u + 1) * CHUNK], y_bf, 1, HALF + u * CHUNK, CHUNK)
-        nc.sync.dma_start(words_out[:, 1, HALF:], y_codes[1][1][:])
+            first = HALF + u * CHUNK
+            codes = y_codes[1][1][:, u * CHUNK : (u + 1) * CHUNK]
+            quantise(codes, y_bf, 1, first, CHUNK)
+            nc.sync.dma_start(words_out[:, 1, first : first + CHUNK], codes)
         for q in range(QUADS):
             queue = nc.sync if q % 2 == 0 else nc.scalar
             queue.dma_start(

@@ -36,7 +36,7 @@ def tile_list_modal_operator_query_kernel(
 
     with ExitStack() as ctx:
         keep = ctx.enter_context(tc.tile_pool(name="keep", bufs=1))
-        psum = ctx.enter_context(tc.psum_pool(name="psum", bufs=4))
+        psum = ctx.enter_context(tc.psum_pool(name="psum", bufs=1))
 
         def sb(shape, dtype, name, after=None):
             return keep.tile(shape, dtype, name=name, tag=after or name, align_bytes=64)
@@ -109,8 +109,8 @@ def tile_list_modal_operator_query_kernel(
         resp = [[sb([P, HALF], F32, "resp%d_%d" % (t, h)) for h in range(2)] for t in range(PACK - 1)]
         held = []
         in_order = [(h, t) for h in range(2) for t in range(2)] + [(h, t) for t in (2, 3) for h in range(2)]
-        for h, t in in_order:
-            acc = psum.tile([P, HALF], F32, name="acc", tag="acc")
+        for n, (h, t) in enumerate(in_order):
+            acc = psum.tile([P, HALF], F32, name="acc", tag="bank%d" % (n % 4))
             for a in range(passes):
                 col = a * H + t * P
                 nc.tensor.matmul_mx(
@@ -130,11 +130,11 @@ def tile_list_modal_operator_query_kernel(
         gT_rows = gT.rearrange("(p t) n -> t p n", t=PACK)
         w2_rows = w2.rearrange("(a p i) r -> a p i r", a=passes, i=PACK)
         trunk = [
-            sb([P, T], F32, "trunk%d" % t, after) for t, after in enumerate(("tab_sc", "w1_raw", "tab1", "w1_sc"))
+            sb([P, T], F32, "trunk%d" % t, after) for t, after in enumerate(("tab_sc", "w1_raw", "tab0", "w1_sc"))
         ]
-        w2_first = sb([P, PACK, H], F32, "w2_first", "tab0")
+        w2_first = sb([P, PACK, H], F32, "w2_first", "sc_raw")
         w2_second = [
-            sb([P, PACK, H // 2], F32, "w2_second%d" % u, after) for u, after in enumerate(("picked_sc", "w1_codes"))
+            sb([P, PACK, H // 2], F32, "w2_second%d" % u, after) for u, after in enumerate(("picked_sc", "tab1"))
         ]
         wb_raw = [sb([P, KP], I32, "wb_raw%d" % g, "resp0_%d" % g) for g in range(groups)]
         mean = sb([P, groups, PACK], F32, "mean", "resp1_1")
@@ -150,17 +150,29 @@ def tile_list_modal_operator_query_kernel(
             nc.sync.dma_start(wb_raw[g][:], wb_cols[:, g * KP : (g + 1) * KP])
         nc.sync.dma_start(mean[:], ymean.rearrange("(g p t) -> p g t", g=groups, t=PACK))
 
-        gated_rows = sb([P, 2 * PACK - 1, HALF], F32, "gated_rows")
-        gated = [gated_rows[:, PACK - 1 :, :], gated_rows[:, :PACK, :]]
+        parts = ((0, CHUNK), (CHUNK, CHUNK), (HALF, HALF))
+        gated_rows = sb([P, 28 * BLOCK], F32, "gated_rows")
+        gated = [
+            gated_rows[:, base : base + PACK * count].rearrange("p (t j) -> p t j", t=PACK)
+            for base, (first, count) in zip((20 * BLOCK, 13 * BLOCK, 0), parts)
+        ]
+
+        def part_of(first):
+            part = min(first // CHUNK, 2)
+            return part, first - parts[part][0]
 
         def gate(t, first, count, response):
-            h, j0 = divmod(first, HALF)
+            part, j0 = part_of(first)
             nc.vector.tensor_tensor(
-                gated[h][:, t, j0 : j0 + count], trunk[t][:].indirect(list_cols(first, count)), response, MULT
+                gated[part][:, t, j0 : j0 + count], trunk[t][:].indirect(list_cols(first, count)), response, MULT
             )
 
         for h, t in in_order[:-2]:
-            gate(t, h * HALF, HALF, resp[t][h][:])
+            if h == 0:
+                for first in (0, CHUNK):
+                    gate(t, first, CHUNK, resp[t][h][:, first : first + CHUNK])
+            else:
+                gate(t, HALF, HALF, resp[t][h][:])
         wb_sc = sb([P, KP], U8, "wb_sc", "resp1_0")
         nc.vector.tensor_copy(
             wb_sc[:].rearrange("p (t m) -> p t m", t=PACK),
@@ -180,61 +192,32 @@ def tile_list_modal_operator_query_kernel(
             w2_sc.append(sb([P, H], U8, "w2_sc%d" % a))
             nc.vector.quantize_mx(w2_codes[a][:].bitcast(FP8X4), w2_sc[a][:], grouped[:])
 
-        last_resp = sb([P, 2, HALF], F32, "last_resp", "w1_codes")
-        for h, count in enumerate((CHUNK, HALF)):
-            nc.scalar.activation(last_resp[:, h, :count], held[h][:, :count], ACT.Tanh, bias=bias1[:, PACK - 1 :])
+        last_resp = []
+        for (first, count), after in zip(parts, ("tab1", "picked_sc", "sc_raw")):
+            last_resp.append(sb([P, count], F32, "last_resp%d" % first, after))
+            j0 = first % HALF
+            nc.scalar.activation(
+                last_resp[-1][:], held[first // HALF][:, j0 : j0 + count], ACT.Tanh, bias=bias1[:, PACK - 1 :]
+            )
 
         c_codes, c_sc = [], []
-        wb_codes = [sb([P, KP], I32, "wb_codes%d" % g) for g in range(groups)]
-        for chunk, (first, width) in enumerate(SPANS):
-            h = first // HALF
-            if first == CHUNK:
-                late = sb([P, CHUNK], F32, "resp_late", "resp0_0")
-                nc.scalar.activation(late[:], held[0][:, CHUNK:], ACT.Tanh, bias=bias1[:, PACK - 1 :])
-                response = late[:]
-            else:
-                response = last_resp[:, h, first % HALF : first % HALF + width]
-            gate(PACK - 1, first, width, response)
-            c_bf = sb([P, width, PACK], BF16, "c_bf%d" % chunk)
-            for w in range(width // BLOCK):
-                j0 = first % HALF + w * BLOCK
-                lin = psum.tile([P, PACK, BLOCK], F32, name="lin", tag="lin")
-                for a in range(passes):
-                    for t in range(PACK):
-                        nc.tensor.matmul_mx(
-                            lin[:, t, :],
-                            lhsT=w2_codes[a][:, t * P : (t + 1) * P].bitcast(FP8X4),
-                            lhsT_scale=w2_sc[a][:, t * P : (t + 1) * P],
-                            rhs=v[a][h][:, j0 : j0 + BLOCK].bitcast(FP8X4),
-                            rhs_scale=v_sc[a][:, h * HALF + j0 : h * HALF + j0 + BLOCK],
-                            start=(a == 0 and t == 0),
-                            stop=(a == passes - 1 and t == PACK - 1),
-                        )
-                nc.vector.tensor_tensor(
-                    c_bf[:, w * BLOCK : (w + 1) * BLOCK, :].rearrange("p (c i) t -> p c t i", i=4),
-                    lin[:].rearrange("p t (c i) -> p c t i", i=4),
-                    gated[h][:, :, j0 : j0 + BLOCK].rearrange("p t (c i) -> p c t i", i=4),
-                    MULT,
-                )
-            c_codes.append(sb([P, width], U32, "c_codes%d" % chunk))
-            c_sc.append(sb([P, width], U8, "c_sc%d" % chunk))
-            nc.vector.quantize_mx(
-                c_codes[chunk][:].bitcast(FP8X4), c_sc[chunk][:], c_bf[:].rearrange("p j t -> p (j t)")
+        wb_codes = []
+
+        def deal_wb(after):
+            g = len(wb_codes)
+            wb_codes.append(sb([P, KP], I32, "wb_codes%d" % g, after))
+            nc.gpsimd.tensor_copy(
+                wb_codes[g][:].rearrange("p (t m) -> p t m", t=PACK),
+                wb_raw[g][:].rearrange("p (m t) -> p t m", t=PACK),
             )
-            if chunk == 0:
-                for g in range(groups):
-                    nc.vector.tensor_copy(
-                        wb_codes[g][:].rearrange("p (t m i) -> p m t i", t=PACK, i=4),
-                        wb_raw[g][:].rearrange("p (m i t) -> p m t i", t=PACK, i=4),
-                    )
 
         y = [[sb([P, PACK, HALF], F32, "y%d_%d" % (h, g)) for g in range(groups)] for h in range(2)]
 
-        def y_bank(chunk, g, t0):
+        def y_bank(chunk, g, t0, bank):
             first, width = SPANS[chunk]
             h, j0 = divmod(first, HALF)
             per_bank = BANK // width
-            acc = psum.tile([P, per_bank, width], F32, name="acc", tag="acc")
+            acc = psum.tile([P, per_bank, width], F32, name="acc", tag="bank%d" % bank)
             for s in range(per_bank):
                 col = (t0 + s) * P
                 nc.tensor.matmul_mx(
@@ -277,18 +260,61 @@ def tile_list_modal_operator_query_kernel(
             )
 
         on_vector, on_scalar = nc.vector.tensor_copy, nc.scalar.copy
-        for chunk, (first, width) in enumerate(SPANS[:3]):
-            if first == CHUNK:
-                early = weave(on_scalar, 0, 0, CHUNK)
-            for g in range(groups):
-                for t0 in range(0, PACK, BANK // width):
-                    y_bank(chunk, g, t0)
-                store(nc.sync, g, 0, PACK, first, width)
+
+        def first_half(g, chunk):
+            first, width = SPANS[chunk]
+            for t0 in range(0, PACK, BANK // width):
+                y_bank(chunk, g, t0, 6 * g + chunk if chunk < 2 else 6 * (1 - g) + t0 // 2)
+            store(nc.sync, g, 0, PACK, first, width)
+
+        for chunk, (first, width) in enumerate(SPANS):
+            h = first // HALF
+            part, g0 = part_of(first)
+            if chunk == 0:
+                for j0 in (0, BLOCK):
+                    gate(PACK - 1, j0, BLOCK, last_resp[0][:, j0 : j0 + BLOCK])
+                deal_wb("tab1")
+            if chunk >= 2:
+                gate(PACK - 1, first, width, last_resp[part][:, g0 : g0 + width])
+            if chunk == 2:
+                deal_wb("picked_sc")
+            c_bf = sb([P, width, PACK], BF16, "c_bf%d" % chunk)
+            for w in range(width // BLOCK):
+                j0 = first % HALF + w * BLOCK
+                lin = psum.tile([P, PACK, BLOCK], F32, name="lin", tag="bank%d" % (2 + (2 + first // BLOCK + w) % 6))
+                for a in range(passes):
+                    for t in range(PACK):
+                        nc.tensor.matmul_mx(
+                            lin[:, t, :],
+                            lhsT=w2_codes[a][:, t * P : (t + 1) * P].bitcast(FP8X4),
+                            lhsT_scale=w2_sc[a][:, t * P : (t + 1) * P],
+                            rhs=v[a][h][:, j0 : j0 + BLOCK].bitcast(FP8X4),
+                            rhs_scale=v_sc[a][:, h * HALF + j0 : h * HALF + j0 + BLOCK],
+                            start=(a == 0 and t == 0),
+                            stop=(a == passes - 1 and t == PACK - 1),
+                        )
+                nc.vector.tensor_tensor(
+                    c_bf[:, w * BLOCK : (w + 1) * BLOCK, :].rearrange("p (c i) t -> p c t i", i=4),
+                    lin[:].rearrange("p t (c i) -> p c t i", i=4),
+                    gated[part][:, :, g0 + w * BLOCK : g0 + (w + 1) * BLOCK].rearrange("p t (c i) -> p c t i", i=4),
+                    MULT,
+                )
+            c_codes.append(sb([P, width], U32, "c_codes%d" % chunk))
+            c_sc.append(sb([P, width], U8, "c_sc%d" % chunk))
+            nc.vector.quantize_mx(
+                c_codes[chunk][:].bitcast(FP8X4), c_sc[chunk][:], c_bf[:].rearrange("p j t -> p (j t)")
+            )
+            if chunk < 2:
+                first_half(0, chunk)
+            if chunk == 2:
+                for g, done in ((1, 0), (1, 1), (0, 2), (1, 2)):
+                    first_half(g, done)
+
         last_chunk = len(SPANS) - 1
         for g in range(groups):
             for chunk in (last_chunk - 1, last_chunk):
                 for t0 in range(0, PACK, BANK // CHUNK):
-                    y_bank(chunk, g, t0)
+                    y_bank(chunk, g, t0, 6 * (last_chunk - chunk) + t0 // 2)
                     if chunk == last_chunk:
                         store(nc.scalar, g, t0, t0 + BANK // CHUNK, HALF, HALF)
 
@@ -296,9 +322,7 @@ def tile_list_modal_operator_query_kernel(
             [sb([P, HALF], I32, "y_codes%d_%d" % (h, g), "w1_sc" if h + g == 0 else None) for g in range(groups)]
             for h in range(2)
         ]
-        rest = weave(on_vector, 0, CHUNK, CHUNK, "c_bf%d" % last_chunk)
-        quantise(y_codes[0][0][:, CHUNK:], rest, 0, CHUNK, CHUNK)
-        quantise(y_codes[0][0][:, :CHUNK], early, 0, 0, CHUNK)
+        quantise(y_codes[0][0][:], weave(on_vector, 0, 0, HALF, "c_bf%d" % last_chunk), 0, 0, HALF)
         nc.sync.dma_start(words_out[:, 0, :HALF], y_codes[0][0][:])
         quantise(y_codes[0][1][:], weave(on_vector, 1, 0, HALF, "gated_rows"), 1, 0, HALF)
         nc.sync.dma_start(words_out[:, 1, :HALF], y_codes[0][1][:])

@@ -207,8 +207,8 @@ def tile_list_modal_operator_query_kernel(
             g = len(wb_codes)
             wb_codes.append(sb([P, KP], I32, "wb_codes%d" % g, after))
             nc.gpsimd.tensor_copy(
-                wb_codes[g][:].rearrange("p (t m) -> p t m", t=PACK),
-                wb_raw[g][:].rearrange("p (m t) -> p t m", t=PACK),
+                wb_codes[g][:].rearrange("p (t m i) -> p m t i", t=PACK, i=4),
+                wb_raw[g][:].rearrange("p (m i t) -> p m t i", t=PACK, i=4),
             )
 
         y = [[sb([P, PACK, HALF], F32, "y%d_%d" % (h, g)) for g in range(groups)] for h in range(2)]

@@ -211,11 +211,10 @@ def tile_list_modal_operator_query_kernel(
                 wb_raw[g][:].rearrange("p (m i t) -> p m t i", t=PACK, i=4),
             )
 
-        y = [[sb([P, PACK, HALF], F32, "y%d_%d" % (h, g)) for g in range(groups)] for h in range(2)]
+        y = [sb([P, PACK, S], F32, "y%d" % g) for g in range(groups)]
 
         def y_bank(chunk, g, t0, bank):
             first, width = SPANS[chunk]
-            h, j0 = divmod(first, HALF)
             per_bank = BANK // width
             acc = psum.tile([P, per_bank, width], F32, name="acc", tag="bank%d" % bank)
             for s in range(per_bank):
@@ -232,23 +231,21 @@ def tile_list_modal_operator_query_kernel(
             for s in range(per_bank):
                 t = t0 + s
                 nc.scalar.activation(
-                    y[h][g][:, t, j0 : j0 + width], acc[:, s, :], ACT.Identity, bias=mean[:, g, t : t + 1]
+                    y[g][:, t, first : first + width], acc[:, s, :], ACT.Identity, bias=mean[:, g, t : t + 1]
                 )
 
         def store(queue, g, t0, t1, first, width):
-            h, j0 = divmod(first, HALF)
             rows = out_0[g * KP : (g + 1) * KP, first : first + width].rearrange("(p t) j -> p t j", t=PACK)
-            queue.dma_start(rows[:, t0:t1, :], y[h][g][:, t0:t1, j0 : j0 + width])
+            queue.dma_start(rows[:, t0:t1, :], y[g][:, t0:t1, first : first + width])
 
         y_sc = sb([P, groups * S], U8, "y_sc")
         words_out = out_1.rearrange("g p j t -> p g (j t)").bitcast(I32)
 
         def weave(engine_copy, g, first, width, after=None):
-            h, j0 = divmod(first, HALF)
             y_bf = sb([P, width, PACK], BF16, "y_bf%d_%d" % (first, g), after)
             engine_copy(
                 y_bf[:].rearrange("p (c i) t -> p c t i", i=4),
-                y[h][g][:, :, j0 : j0 + width].rearrange("p t (c i) -> p c t i", i=4),
+                y[g][:, :, first : first + width].rearrange("p t (c i) -> p c t i", i=4),
             )
             return y_bf
 
@@ -261,11 +258,14 @@ def tile_list_modal_operator_query_kernel(
 
         on_vector, on_scalar = nc.vector.tensor_copy, nc.scalar.copy
 
-        def first_half(g, chunk):
+        def y_chunk(g, chunk, bank, queue=None, joined=False):
             first, width = SPANS[chunk]
             for t0 in range(0, PACK, BANK // width):
-                y_bank(chunk, g, t0, 6 * g + chunk if chunk < 2 else 6 * (1 - g) + t0 // 2)
-            store(nc.sync, g, 0, PACK, first, width)
+                y_bank(chunk, g, t0, bank + t0 // 2)
+                if joined:
+                    store(queue, g, t0, t0 + 2, first - width, 2 * width)
+            if queue is not None and not joined:
+                store(queue, g, 0, PACK, first, width)
 
         for chunk, (first, width) in enumerate(SPANS):
             h = first // HALF
@@ -305,18 +305,18 @@ def tile_list_modal_operator_query_kernel(
                 c_codes[chunk][:].bitcast(FP8X4), c_sc[chunk][:], c_bf[:].rearrange("p j t -> p (j t)")
             )
             if chunk < 2:
-                first_half(0, chunk)
+                y_chunk(0, chunk, chunk, nc.sync)
             if chunk == 2:
-                for g, done in ((1, 0), (1, 1), (0, 2), (1, 2)):
-                    first_half(g, done)
+                y_chunk(1, 0, 6, nc.sync)
+                y_chunk(1, 1, 7, nc.sync)
+                y_chunk(1, 2, 6, nc.sync)
+                y_chunk(0, 2, 0)
 
         last_chunk = len(SPANS) - 1
-        for g in range(groups):
-            for chunk in (last_chunk - 1, last_chunk):
-                for t0 in range(0, PACK, BANK // CHUNK):
-                    y_bank(chunk, g, t0, 6 * (last_chunk - chunk) + t0 // 2)
-                    if chunk == last_chunk:
-                        store(nc.scalar, g, t0, t0 + BANK // CHUNK, HALF, HALF)
+        y_chunk(0, 3, 6, nc.sync, True)
+        y_chunk(0, 4, 0, nc.scalar)
+        y_chunk(1, 3, 6)
+        y_chunk(1, 4, 0, nc.scalar, True)
 
         y_codes = [
             [sb([P, HALF], I32, "y_codes%d_%d" % (h, g), "w1_sc" if h + g == 0 else None) for g in range(groups)]

@@ -25,6 +25,10 @@ HALF = S // 2
 BLOCK = BANK // PACK
 CHUNK = 256
 SPANS = ((0, BLOCK), (BLOCK, BLOCK), (CHUNK, CHUNK), (2 * CHUNK, CHUNK), (3 * CHUNK, CHUNK))
+PAIR = BANK // CHUNK
+W1_BANKS = 4
+W2_BANKS = (4, 5, 6, 7, 2, 3, 4, 5)
+LOW, HIGH = 0, 6
 
 
 def tile_list_modal_operator_query_kernel(
@@ -40,6 +44,9 @@ def tile_list_modal_operator_query_kernel(
 
         def sb(shape, dtype, name, after=None):
             return keep.tile(shape, dtype, name=name, tag=after or name, align_bytes=64)
+
+        def bank_tile(shape, bank):
+            return psum.tile(shape, F32, name="sums", tag="bank%d" % bank)
 
         offsets = keep.tile([P, S // 16], U16, name="offsets")
         tab_sc = sb([P, T], U8, "tab_sc")
@@ -110,7 +117,7 @@ def tile_list_modal_operator_query_kernel(
         held = []
         in_order = [(h, t) for h in range(2) for t in range(2)] + [(h, t) for t in (2, 3) for h in range(2)]
         for n, (h, t) in enumerate(in_order):
-            acc = psum.tile([P, HALF], F32, name="acc", tag="bank%d" % (n % 4))
+            acc = bank_tile([P, HALF], n % W1_BANKS)
             for a in range(passes):
                 col = a * H + t * P
                 nc.tensor.matmul_mx(
@@ -151,14 +158,16 @@ def tile_list_modal_operator_query_kernel(
         nc.sync.dma_start(mean[:], ymean.rearrange("(g p t) -> p g t", g=groups, t=PACK))
 
         parts = ((0, CHUNK), (CHUNK, CHUNK), (HALF, HALF))
-        gated_rows = sb([P, 28 * BLOCK], F32, "gated_rows")
+        second_at = (PACK - 1) * HALF + BLOCK
+        first_at = second_at + PACK * CHUNK - BLOCK
+        gated_rows = sb([P, first_at + PACK * CHUNK], F32, "gated_rows")
         gated = [
             gated_rows[:, base : base + PACK * count].rearrange("p (t j) -> p t j", t=PACK)
-            for base, (first, count) in zip((20 * BLOCK, 13 * BLOCK, 0), parts)
+            for base, (first, count) in zip((first_at, second_at, 0), parts)
         ]
 
         def part_of(first):
-            part = min(first // CHUNK, 2)
+            part = min(first // CHUNK, len(parts) - 1)
             return part, first - parts[part][0]
 
         def gate(t, first, count, response):
@@ -167,7 +176,7 @@ def tile_list_modal_operator_query_kernel(
                 gated[part][:, t, j0 : j0 + count], trunk[t][:].indirect(list_cols(first, count)), response, MULT
             )
 
-        for h, t in in_order[:-2]:
+        for h, t in in_order[: -len(held)]:
             if h == 0:
                 for first in (0, CHUNK):
                     gate(t, first, CHUNK, resp[t][h][:, first : first + CHUNK])
@@ -200,8 +209,7 @@ def tile_list_modal_operator_query_kernel(
                 last_resp[-1][:], held[first // HALF][:, j0 : j0 + count], ACT.Tanh, bias=bias1[:, PACK - 1 :]
             )
 
-        c_codes, c_sc = [], []
-        wb_codes = []
+        c_codes, c_sc, wb_codes = [], [], []
 
         def deal_wb(after):
             g = len(wb_codes)
@@ -216,7 +224,7 @@ def tile_list_modal_operator_query_kernel(
         def y_bank(chunk, g, t0, bank):
             first, width = SPANS[chunk]
             per_bank = BANK // width
-            acc = psum.tile([P, per_bank, width], F32, name="acc", tag="bank%d" % bank)
+            acc = bank_tile([P, per_bank, width], bank)
             for s in range(per_bank):
                 col = (t0 + s) * P
                 nc.tensor.matmul_mx(
@@ -256,32 +264,32 @@ def tile_list_modal_operator_query_kernel(
                 y_bf[:].rearrange("p j t -> p (j t)"),
             )
 
-        on_vector, on_scalar = nc.vector.tensor_copy, nc.scalar.copy
-
-        def y_chunk(g, chunk, bank, queue=None, joined=False):
+        def y_chunk(g, chunk, bank, queue=None, joined=0):
             first, width = SPANS[chunk]
             for t0 in range(0, PACK, BANK // width):
-                y_bank(chunk, g, t0, bank + t0 // 2)
+                y_bank(chunk, g, t0, bank + t0 // PAIR)
                 if joined:
-                    store(queue, g, t0, t0 + 2, first - width, 2 * width)
+                    store(queue, g, t0, t0 + PAIR, first - joined, joined + width)
             if queue is not None and not joined:
                 store(queue, g, 0, PACK, first, width)
 
         for chunk, (first, width) in enumerate(SPANS):
             h = first // HALF
-            part, g0 = part_of(first)
-            if chunk == 0:
+            part, in_part = part_of(first)
+            narrow = width == BLOCK
+            if first == 0:
                 for j0 in (0, BLOCK):
                     gate(PACK - 1, j0, BLOCK, last_resp[0][:, j0 : j0 + BLOCK])
                 deal_wb("tab1")
-            if chunk >= 2:
-                gate(PACK - 1, first, width, last_resp[part][:, g0 : g0 + width])
-            if chunk == 2:
+            if not narrow:
+                gate(PACK - 1, first, width, last_resp[part][:, in_part : in_part + width])
+            if first == CHUNK:
                 deal_wb("picked_sc")
             c_bf = sb([P, width, PACK], BF16, "c_bf%d" % chunk)
             for w in range(width // BLOCK):
                 j0 = first % HALF + w * BLOCK
-                lin = psum.tile([P, PACK, BLOCK], F32, name="lin", tag="bank%d" % (2 + (2 + first // BLOCK + w) % 6))
+                j1 = in_part + w * BLOCK
+                lin = bank_tile([P, PACK, BLOCK], W2_BANKS[first // BLOCK + w])
                 for a in range(passes):
                     for t in range(PACK):
                         nc.tensor.matmul_mx(
@@ -296,7 +304,7 @@ def tile_list_modal_operator_query_kernel(
                 nc.vector.tensor_tensor(
                     c_bf[:, w * BLOCK : (w + 1) * BLOCK, :].rearrange("p (c i) t -> p c t i", i=4),
                     lin[:].rearrange("p t (c i) -> p c t i", i=4),
-                    gated[part][:, :, g0 + w * BLOCK : g0 + (w + 1) * BLOCK].rearrange("p t (c i) -> p c t i", i=4),
+                    gated[part][:, :, j1 : j1 + BLOCK].rearrange("p t (c i) -> p c t i", i=4),
                     MULT,
                 )
             c_codes.append(sb([P, width], U32, "c_codes%d" % chunk))
@@ -304,38 +312,35 @@ def tile_list_modal_operator_query_kernel(
             nc.vector.quantize_mx(
                 c_codes[chunk][:].bitcast(FP8X4), c_sc[chunk][:], c_bf[:].rearrange("p j t -> p (j t)")
             )
-            if chunk < 2:
-                y_chunk(0, chunk, chunk, nc.sync)
-            if chunk == 2:
-                y_chunk(1, 0, 6, nc.sync)
-                y_chunk(1, 1, 7, nc.sync)
-                y_chunk(1, 2, 6, nc.sync)
-                y_chunk(0, 2, 0)
+            if narrow:
+                y_chunk(0, chunk, LOW + chunk, nc.sync)
+            if first == CHUNK:
+                y_chunk(1, 0, HIGH, nc.sync)
+                y_chunk(1, 1, HIGH + 1)
+                y_chunk(1, 2, HIGH, nc.sync, BLOCK)
 
-        last_chunk = len(SPANS) - 1
-        y_chunk(0, 3, 6, nc.sync, True)
-        y_chunk(0, 4, 0, nc.scalar)
-        y_chunk(1, 3, 6)
-        y_chunk(1, 4, 0, nc.scalar, True)
+        for t0 in range(0, PACK, PAIR):
+            y_bank(2, 0, t0, LOW + t0 // PAIR)
+            y_bank(3, 0, t0, HIGH + t0 // PAIR)
+            store(nc.sync, 0, t0, t0 + PAIR, CHUNK, 2 * CHUNK)
+        y_chunk(0, 4, LOW, nc.scalar)
+        y_chunk(1, 3, HIGH)
+        y_chunk(1, 4, LOW, nc.scalar, CHUNK)
 
-        y_codes = [
-            [sb([P, HALF], I32, "y_codes%d_%d" % (h, g), "w1_sc" if h + g == 0 else None) for g in range(groups)]
-            for h in range(2)
-        ]
-        quantise(y_codes[0][0][:], weave(on_vector, 0, 0, HALF, "c_bf%d" % last_chunk), 0, 0, HALF)
-        nc.sync.dma_start(words_out[:, 0, :HALF], y_codes[0][0][:])
-        quantise(y_codes[0][1][:], weave(on_vector, 1, 0, HALF, "gated_rows"), 1, 0, HALF)
-        nc.sync.dma_start(words_out[:, 1, :HALF], y_codes[0][1][:])
-        quantise(y_codes[1][0][:], weave(on_vector, 0, HALF, HALF), 0, HALF, HALF)
-        nc.sync.dma_start(words_out[:, 0, HALF:], y_codes[1][0][:])
+        on_vector, on_scalar = nc.vector.tensor_copy, nc.scalar.copy
+        y_codes = [sb([P, S], I32, "y_codes%d" % g, after) for g, after in enumerate(("w1_sc", None))]
+        quantise(y_codes[0][:, :HALF], weave(on_vector, 0, 0, HALF, "c_bf%d" % (len(SPANS) - 1)), 0, 0, HALF)
+        quantise(y_codes[1][:, :HALF], weave(on_vector, 1, 0, HALF, "gated_rows"), 1, 0, HALF)
+        nc.sync.dma_start(words_out[:, 1, :HALF], y_codes[1][:, :HALF])
+        quantise(y_codes[0][:, HALF:], weave(on_vector, 0, HALF, HALF), 0, HALF, HALF)
+        nc.sync.dma_start(words_out[:, 0, :], y_codes[0][:])
         tail = [
             weave(engine_copy, 1, HALF + u * CHUNK, CHUNK) for u, engine_copy in enumerate((on_vector, on_scalar))
         ]
         for u, y_bf in enumerate(tail):
             first = HALF + u * CHUNK
-            codes = y_codes[1][1][:, u * CHUNK : (u + 1) * CHUNK]
-            quantise(codes, y_bf, 1, first, CHUNK)
-            nc.sync.dma_start(words_out[:, 1, first : first + CHUNK], codes)
+            quantise(y_codes[1][:, first : first + CHUNK], y_bf, 1, first, CHUNK)
+        nc.sync.dma_start(words_out[:, 1, HALF:], y_codes[1][:, HALF:])
         for q in range(QUADS):
             queue = nc.sync if q % 2 == 0 else nc.scalar
             queue.dma_start(

@@ -40,26 +40,36 @@ def tile_list_modal_operator_query_kernel(
 
     with ExitStack() as ctx:
         keep = ctx.enter_context(tc.tile_pool(name="keep", bufs=1))
+        late = ctx.enter_context(tc.tile_pool(name="late", bufs=1))
         psum = ctx.enter_context(tc.psum_pool(name="psum", bufs=1))
 
         def sb(shape, dtype, name, after=None):
             return keep.tile(shape, dtype, name=name, tag=after or name, align_bytes=64)
 
+        places = {"trunk1": 0, "w2_first": 8192, "w2_second0": 16384, "trunk2": 20480, "w2_second1": 28672,
+                  "trunk3": 32768, "wb_raw0": 40960, "wb_raw1": 43008, "mean": 45056}
+
+        def late_tile(shape, dtype, name, place=None):
+            place = place or name
+            return late.tile(shape, dtype, name=name, tag=place, align_bytes=64, offset=places[place])
+
         def bank_tile(shape, bank):
             return psum.tile(shape, F32, name="sums", tag="bank%d" % bank)
 
         offsets = keep.tile([P, S // 16], U16, name="offsets")
-        tab_sc = sb([P, T], U8, "tab_sc")
+        room = late.tile([P, places["mean"] + 64], U8, name="room", align_bytes=64, offset=0)
+        tab_sc = room[:, :T]
         picked_sc = sb([P, S], U8, "picked_sc")
-        v_sc = [sb([P, S], U8, "v_sc%d" % a) for a in range(passes)]
+        moved_sc = sb([P, S], U8, "moved_sc")
+        v_sc = [picked_sc, moved_sc]
         sc_raw = sb([P, passes * H], U8, "sc_raw")
         w1_raw = sb([P, passes * 2 * H], U8, "w1_raw")
         tab = [sb([P, T], I32, "tab%d" % a) for a in range(passes)]
         bias1 = sb([P, PACK], F32, "bias1")
 
-        nc.gpsimd.memset(sc_raw[:].bitcast(I32), 0)
-        for row0, row1 in ((0, 16), (32, 48), (64, P)):
-            nc.vector.memset(tab_sc[row0:row1, :].bitcast(I32), 0)
+        nc.gpsimd.memset(tab_sc[:112, :].bitcast(I32), 0)
+        nc.vector.memset(sc_raw[:].bitcast(I32), 0)
+        nc.vector.memset(moved_sc[:].bitcast(I32), 0)
 
         wb_sc_raw = sb([P, KP], U8, "wb_sc_raw")
         nc.gpsimd.memset(wb_sc_raw[:].bitcast(I32), 0)
@@ -70,40 +80,44 @@ def tile_list_modal_operator_query_kernel(
             )
 
         nc.sync.dma_start(offsets[:], offs)
-        tab_sc_rows = tab_scales.bitcast(I32).rearrange("a (u o r) t -> o (a u) r t", u=2, o=2)
-        for odd in range(2):
-            nc.sync.dma_start(tab_sc[32 * odd + 16 : 32 * odd + 32, :].bitcast(I32), tab_sc_rows[odd])
-        nc.sync.dma_start(tab[0][:], tab_words[0].rearrange("p n i -> p (n i)").bitcast(I32))
         nc.sync.dma_start(
             w1_raw[:].bitcast(I32).rearrange("p (a n) -> p a n", a=passes),
             w1_words.bitcast(I32).rearrange("a p n -> p a n"),
         )
-        nc.sync.dma_start(bias1[:], b1.rearrange("(p t) -> p t", t=PACK))
+        nc.sync.dma_start(tab_sc[112:, :].bitcast(I32), tab_scales[1].bitcast(I32))
+        for q in range(QUADS):
+            nc.sync.dma_start(
+                tab_sc[32 * q : 32 * q + 4, :].bitcast(I32), tab_scales[0, 4 * q : 4 * q + 4, :].bitcast(I32)
+            )
+        nc.sync.dma_start(tab[0][:], tab_words[0].rearrange("p n i -> p (n i)").bitcast(I32))
         for q in range(QUADS):
             nc.sync.dma_start(
                 sc_raw[32 * q : 32 * q + 4, :].bitcast(I32).rearrange("r (a e) -> r a e", a=passes),
                 w1_scales[:, 4 * q : 4 * q + 4, :].bitcast(I32).rearrange("a r e -> r a e"),
             )
         nc.sync.dma_start(tab[1][:], tab_words[1].rearrange("p n i -> p (n i)").bitcast(I32))
+        nc.sync.dma_start(bias1[:], b1.rearrange("(p t) -> p t", t=PACK))
+        gT_rows = gT.rearrange("(p t) n -> t p n", t=PACK)
+        trunk = [sb([P, T], F32, "trunk0")] + [late_tile([P, T], F32, "trunk%d" % t) for t in range(1, PACK)]
+        nc.sync.dma_start(trunk[0][:], gT_rows[0])
 
-        nc.vector.tensor_copy(picked_sc[:], tab_sc[:].indirect(offsets[:]))
-        for a in reversed(range(passes)):
-            for upper in range(2):
-                row = 16 + 4 * (2 * a + upper)
-                nc.sync.dma_start(
-                    v_sc[a][64 * upper : 64 * upper + 64, :].bitcast(I32), picked_sc[row : row + 64, :].bitcast(I32)
-                )
+        w1_codes = sb([P, passes * 2 * H], U8, "w1_codes")
+        nc.vector.tensor_copy(
+            w1_codes[:].bitcast(U16).rearrange("p (a t m) -> p a t m", a=passes, t=PACK),
+            w1_raw[:].bitcast(U16).rearrange("p (a m t) -> p a t m", a=passes, t=PACK),
+        )
+
+        nc.vector.tensor_copy(picked_sc[:], tab_sc.indirect(offsets[:]))
+        for q in range(QUADS):
+            nc.sync.dma_start(
+                moved_sc[32 * q : 32 * q + 4, :].bitcast(I32), picked_sc[112 + 4 * q : 116 + 4 * q, :].bitcast(I32)
+            )
 
         def list_cols(first, count):
             return offsets[:, first // 16 : (first + count) // 16]
 
         v = [[sb([P, HALF], U32, "v%d_%d" % (a, h)) for h in range(2)] for a in range(passes)]
         nc.vector.tensor_copy(v[0][0][:], tab[0][:].bitcast(U32).indirect(list_cols(0, HALF)))
-        w1_codes = sb([P, passes * 2 * H], U8, "w1_codes")
-        nc.vector.tensor_copy(
-            w1_codes[:].bitcast(U16).rearrange("p (a t m) -> p a t m", a=passes, t=PACK),
-            w1_raw[:].bitcast(U16).rearrange("p (a m t) -> p a t m", a=passes, t=PACK),
-        )
         w1_sc = sb([P, passes * H], U8, "w1_sc")
         nc.vector.tensor_copy(
             w1_sc[:].rearrange("p (a t m) -> p a t m", a=passes, t=PACK),
@@ -134,18 +148,11 @@ def tile_list_modal_operator_query_kernel(
             else:
                 nc.scalar.activation(resp[t][h][:], acc[:], ACT.Tanh, bias=bias1[:, t : t + 1])
 
-        gT_rows = gT.rearrange("(p t) n -> t p n", t=PACK)
         w2_rows = w2.rearrange("(a p i) r -> a p i r", a=passes, i=PACK)
-        trunk = [
-            sb([P, T], F32, "trunk%d" % t, after) for t, after in enumerate(("tab_sc", "w1_raw", "tab0", "w1_sc"))
-        ]
-        w2_first = sb([P, PACK, H], F32, "w2_first", "sc_raw")
-        w2_second = [
-            sb([P, PACK, H // 2], F32, "w2_second%d" % u, after) for u, after in enumerate(("picked_sc", "tab1"))
-        ]
-        wb_raw = [sb([P, KP], I32, "wb_raw%d" % g, "resp0_%d" % g) for g in range(groups)]
-        mean = sb([P, groups, PACK], F32, "mean", "resp1_1")
-        nc.sync.dma_start(trunk[0][:], gT_rows[0])
+        w2_first = late_tile([P, PACK, H], F32, "w2_first")
+        w2_second = [late_tile([P, PACK, H // 2], F32, "w2_second%d" % u) for u in range(2)]
+        wb_raw = [late_tile([P, KP], I32, "wb_raw%d" % g) for g in range(groups)]
+        mean = late_tile([P, groups, PACK], F32, "mean")
         nc.sync.dma_start(trunk[1][:], gT_rows[1])
         nc.sync.dma_start(w2_first[:], w2_rows[0])
         nc.sync.dma_start(w2_second[0][:], w2_rows[1][:, :, : H // 2])
@@ -202,8 +209,8 @@ def tile_list_modal_operator_query_kernel(
             nc.vector.quantize_mx(w2_codes[a][:].bitcast(FP8X4), w2_sc[a][:], grouped[:])
 
         last_resp = []
-        for (first, count), after in zip(parts, ("tab1", "picked_sc", "sc_raw")):
-            last_resp.append(sb([P, count], F32, "last_resp%d" % first, after))
+        for (first, count), after in zip(parts, ("w2_second1", "w2_second0", "w2_first")):
+            last_resp.append(late_tile([P, count], F32, "last_resp%d" % first, after))
             j0 = first % HALF
             nc.scalar.activation(
                 last_resp[-1][:], held[first // HALF][:, j0 : j0 + count], ACT.Tanh, bias=bias1[:, PACK - 1 :]
@@ -213,7 +220,7 @@ def tile_list_modal_operator_query_kernel(
 
         def deal_wb(after):
             g = len(wb_codes)
-            wb_codes.append(sb([P, KP], I32, "wb_codes%d" % g, after))
+            wb_codes.append(late_tile([P, KP], I32, "wb_codes%d" % g, after))
             nc.gpsimd.tensor_copy(
                 wb_codes[g][:].rearrange("p (t m i) -> p m t i", t=PACK, i=4),
                 wb_raw[g][:].rearrange("p (m i t) -> p m t i", t=PACK, i=4),
@@ -280,11 +287,11 @@ def tile_list_modal_operator_query_kernel(
             if first == 0:
                 for j0 in (0, BLOCK):
                     gate(PACK - 1, j0, BLOCK, last_resp[0][:, j0 : j0 + BLOCK])
-                deal_wb("tab1")
+                deal_wb("w2_second1")
             if not narrow:
                 gate(PACK - 1, first, width, last_resp[part][:, in_part : in_part + width])
             if first == CHUNK:
-                deal_wb("picked_sc")
+                deal_wb("w2_second0")
             c_bf = sb([P, width, PACK], BF16, "c_bf%d" % chunk)
             for w in range(width // BLOCK):
                 j0 = first % HALF + w * BLOCK
@@ -328,7 +335,7 @@ def tile_list_modal_operator_query_kernel(
         y_chunk(1, 4, LOW, nc.scalar, CHUNK)
 
         on_vector, on_scalar = nc.vector.tensor_copy, nc.scalar.copy
-        y_codes = [sb([P, S], I32, "y_codes%d" % g, after) for g, after in enumerate(("w1_sc", None))]
+        y_codes = [late_tile([P, S], I32, "y_codes0", "trunk3"), sb([P, S], I32, "y_codes1")]
         quantise(y_codes[0][:, :HALF], weave(on_vector, 0, 0, HALF, "c_bf%d" % (len(SPANS) - 1)), 0, 0, HALF)
         quantise(y_codes[1][:, :HALF], weave(on_vector, 1, 0, HALF, "gated_rows"), 1, 0, HALF)
         nc.sync.dma_start(words_out[:, 1, :HALF], y_codes[1][:, :HALF])

@@ -75,7 +75,7 @@ def tile_list_modal_operator_query_kernel(
         nc.gpsimd.memset(wb_sc_raw[:].bitcast(I32), 0)
         for q in range(QUADS):
             nc.gpsimd.dma_start(
-                wb_sc_raw[32 * q : 32 * q + 8, :].bitcast(I32),
+                wb_sc_raw[32 * q + 8 : 32 * q + 16, :].bitcast(I32),
                 wb_scales[0, 4 * q : 4 * q + 4, :].bitcast(I32).rearrange("r (g e) -> g r e", g=groups),
             )
 
@@ -85,15 +85,13 @@ def tile_list_modal_operator_query_kernel(
             w1_words.bitcast(I32).rearrange("a p n -> p a n"),
         )
         nc.sync.dma_start(tab_sc[112:, :].bitcast(I32), tab_scales[1].bitcast(I32))
-        for q in range(QUADS):
-            nc.sync.dma_start(
-                tab_sc[32 * q : 32 * q + 4, :].bitcast(I32), tab_scales[0, 4 * q : 4 * q + 4, :].bitcast(I32)
-            )
+        for r in range(4):
+            nc.sync.dma_start(tab_sc[r::32, :].bitcast(I32), tab_scales[0, r::4, :].bitcast(I32))
         nc.sync.dma_start(tab[0][:], tab_words[0].rearrange("p n i -> p (n i)").bitcast(I32))
-        for q in range(QUADS):
+        for r in range(4):
             nc.sync.dma_start(
-                sc_raw[32 * q : 32 * q + 4, :].bitcast(I32).rearrange("r (a e) -> r a e", a=passes),
-                w1_scales[:, 4 * q : 4 * q + 4, :].bitcast(I32).rearrange("a r e -> r a e"),
+                sc_raw[r::32, :].bitcast(I32).rearrange("q (a e) -> q a e", a=passes),
+                w1_scales[:, r::4, :].bitcast(I32).rearrange("a q e -> q a e"),
             )
         nc.sync.dma_start(tab[1][:], tab_words[1].rearrange("p n i -> p (n i)").bitcast(I32))
         nc.sync.dma_start(bias1[:], b1.rearrange("(p t) -> p t", t=PACK))
@@ -108,10 +106,8 @@ def tile_list_modal_operator_query_kernel(
         )
 
         nc.vector.tensor_copy(picked_sc[:], tab_sc.indirect(offsets[:]))
-        for q in range(QUADS):
-            nc.sync.dma_start(
-                moved_sc[32 * q : 32 * q + 4, :].bitcast(I32), picked_sc[112 + 4 * q : 116 + 4 * q, :].bitcast(I32)
-            )
+        for r in range(4):
+            nc.sync.dma_start(moved_sc[r::32, :].bitcast(I32), picked_sc[112 + r :: 4, :].bitcast(I32))
 
         def list_cols(first, count):
             return offsets[:, first // 16 : (first + count) // 16]
@@ -237,7 +233,7 @@ def tile_list_modal_operator_query_kernel(
                 nc.tensor.matmul_mx(
                     acc[:, s, :],
                     lhsT=wb_codes[g][:, col : col + P].bitcast(FP8X4),
-                    lhsT_scale=wb_sc[4 * g :, col : col + P],
+                    lhsT_scale=wb_sc[8 + 4 * g :, col : col + P],
                     rhs=c_codes[chunk][:].bitcast(FP8X4),
                     rhs_scale=c_sc[chunk][:],
                     start=True,
@@ -348,9 +344,9 @@ def tile_list_modal_operator_query_kernel(
             first = HALF + u * CHUNK
             quantise(y_codes[1][:, first : first + CHUNK], y_bf, 1, first, CHUNK)
         nc.sync.dma_start(words_out[:, 1, HALF:], y_codes[1][:, HALF:])
-        for q in range(QUADS):
-            queue = nc.sync if q % 2 == 0 else nc.scalar
+        for r in range(4):
+            queue = nc.sync if r % 2 == 0 else nc.scalar
             queue.dma_start(
-                out_2[:, 4 * q : 4 * q + 4, :].bitcast(I32).rearrange("g r j -> r g j"),
-                y_sc[32 * q : 32 * q + 4, :].bitcast(I32).rearrange("r (g j) -> r g j", g=groups),
+                out_2[:, r::4, :].bitcast(I32).rearrange("g q j -> q g j"),
+                y_sc[r::32, :].bitcast(I32).rearrange("q (g j) -> q g j", g=groups),
             )

@@ -28,7 +28,7 @@ SPANS = ((0, BLOCK), (BLOCK, BLOCK), (CHUNK, CHUNK), (2 * CHUNK, CHUNK), (3 * CH
 PAIR = BANK // CHUNK
 W1_BANKS = 4
 W2_BANKS = (4, 5, 6, 7, 2, 3, 4, 5)
-LOW, HIGH = 0, 6
+Y_BANKS = (0, 1, 6, 7)
 
 
 def tile_list_modal_operator_query_kernel(
@@ -224,21 +224,27 @@ def tile_list_modal_operator_query_kernel(
 
         y = [sb([P, PACK, S], F32, "y%d" % g) for g in range(groups)]
 
-        def y_bank(chunk, g, t0, bank):
-            first, width = SPANS[chunk]
+        filled = []
+
+        def y_bank(chunks, g, t0):
+            first = SPANS[chunks[0]][0]
+            width = sum(SPANS[chunk][1] for chunk in chunks)
             per_bank = BANK // width
-            acc = bank_tile([P, per_bank, width], bank)
+            acc = bank_tile([P, per_bank, width], Y_BANKS[len(filled) % len(Y_BANKS)])
+            filled.append(acc)
             for s in range(per_bank):
                 col = (t0 + s) * P
-                nc.tensor.matmul_mx(
-                    acc[:, s, :],
-                    lhsT=wb_codes[g][:, col : col + P].bitcast(FP8X4),
-                    lhsT_scale=wb_sc[8 + 4 * g :, col : col + P],
-                    rhs=c_codes[chunk][:].bitcast(FP8X4),
-                    rhs_scale=c_sc[chunk][:],
-                    start=True,
-                    stop=True,
-                )
+                for chunk in chunks:
+                    j0 = SPANS[chunk][0] - first
+                    nc.tensor.matmul_mx(
+                        acc[:, s, j0 : j0 + SPANS[chunk][1]],
+                        lhsT=wb_codes[g][:, col : col + P].bitcast(FP8X4),
+                        lhsT_scale=wb_sc[8 + 4 * g :, col : col + P],
+                        rhs=c_codes[chunk][:].bitcast(FP8X4),
+                        rhs_scale=c_sc[chunk][:],
+                        start=True,
+                        stop=True,
+                    )
             for s in range(per_bank):
                 t = t0 + s
                 nc.scalar.activation(
@@ -266,15 +272,6 @@ def tile_list_modal_operator_query_kernel(
                 y_sc[:, g * S + first : g * S + first + width],
                 y_bf[:].rearrange("p j t -> p (j t)"),
             )
-
-        def y_chunk(g, chunk, bank, queue=None, joined=0):
-            first, width = SPANS[chunk]
-            for t0 in range(0, PACK, BANK // width):
-                y_bank(chunk, g, t0, bank + t0 // PAIR)
-                if joined:
-                    store(queue, g, t0, t0 + PAIR, first - joined, joined + width)
-            if queue is not None and not joined:
-                store(queue, g, 0, PACK, first, width)
 
         for chunk, (first, width) in enumerate(SPANS):
             h = first // HALF
@@ -316,34 +313,40 @@ def tile_list_modal_operator_query_kernel(
                 c_codes[chunk][:].bitcast(FP8X4), c_sc[chunk][:], c_bf[:].rearrange("p j t -> p (j t)")
             )
             if narrow:
-                y_chunk(0, chunk, LOW + chunk, nc.sync)
+                y_bank([chunk], 0, 0)
+                store(nc.sync, 0, 0, PACK, first, width)
             if first == CHUNK:
-                y_chunk(1, 0, HIGH, nc.sync)
-                y_chunk(1, 1, HIGH + 1)
-                y_chunk(1, 2, HIGH, nc.sync, BLOCK)
+                for chunks, g, start in (([0, 1], 1, 0), ([2], 0, CHUNK)):
+                    for t0 in range(0, PACK, PAIR):
+                        y_bank(chunks, g, t0)
+                        store(nc.sync, g, t0, t0 + PAIR, start, CHUNK)
+                y_bank([2], 1, 0)
+                store(nc.sync, 1, 0, PAIR, CHUNK, CHUNK)
+                y_bank([2], 1, PAIR)
 
-        for t0 in range(0, PACK, PAIR):
-            y_bank(2, 0, t0, LOW + t0 // PAIR)
-            y_bank(3, 0, t0, HIGH + t0 // PAIR)
-            store(nc.sync, 0, t0, t0 + PAIR, CHUNK, 2 * CHUNK)
-        y_chunk(0, 4, LOW, nc.scalar)
-        y_chunk(1, 3, HIGH)
-        y_chunk(1, 4, LOW, nc.scalar, CHUNK)
+        y_bank([3], 1, PAIR)
+        store(nc.sync, 1, PAIR, PACK, CHUNK, HALF)
+        for g, t0, queue in ((1, 0, nc.sync), (0, 0, nc.scalar), (0, PAIR, nc.scalar)):
+            y_bank([3], g, t0)
+            y_bank([4], g, t0)
+            store(queue, g, t0, t0 + PAIR, HALF, HALF)
+        y_bank([4], 1, PAIR)
+        store(nc.scalar, 1, PAIR, PACK, HALF + CHUNK, CHUNK)
 
         on_vector, on_scalar = nc.vector.tensor_copy, nc.scalar.copy
-        y_codes = [late_tile([P, S], I32, "y_codes0", "trunk3"), sb([P, S], I32, "y_codes1")]
-        quantise(y_codes[0][:, :HALF], weave(on_vector, 0, 0, HALF, "c_bf%d" % (len(SPANS) - 1)), 0, 0, HALF)
-        quantise(y_codes[1][:, :HALF], weave(on_vector, 1, 0, HALF, "gated_rows"), 1, 0, HALF)
-        nc.sync.dma_start(words_out[:, 1, :HALF], y_codes[1][:, :HALF])
-        quantise(y_codes[0][:, HALF:], weave(on_vector, 0, HALF, HALF), 0, HALF, HALF)
-        nc.sync.dma_start(words_out[:, 0, :], y_codes[0][:])
-        tail = [
-            weave(engine_copy, 1, HALF + u * CHUNK, CHUNK) for u, engine_copy in enumerate((on_vector, on_scalar))
-        ]
-        for u, y_bf in enumerate(tail):
-            first = HALF + u * CHUNK
-            quantise(y_codes[1][:, first : first + CHUNK], y_bf, 1, first, CHUNK)
-        nc.sync.dma_start(words_out[:, 1, HALF:], y_codes[1][:, HALF:])
+        low_codes = late_tile([P, groups, HALF], I32, "low_codes", "trunk3")
+        high_codes = [sb([P, HALF], I32, "high_codes%d" % g) for g in range(groups)]
+        low = [weave(on_vector, g, 0, HALF, after) for g, after in enumerate(("c_bf4", "gated_rows"))]
+        for g, y_bf in enumerate(low):
+            quantise(low_codes[:, g, :], y_bf, g, 0, HALF)
+        nc.sync.dma_start(words_out[:, :, :HALF], low_codes[:])
+        third = weave(on_vector, 1, HALF, CHUNK)
+        upper = weave(on_vector, 0, HALF, HALF)
+        quantise(high_codes[1][:, :CHUNK], third, 1, HALF, CHUNK)
+        quantise(high_codes[0][:], upper, 0, HALF, HALF)
+        nc.sync.dma_start(words_out[:, 0, HALF:], high_codes[0][:])
+        quantise(high_codes[1][:, CHUNK:], weave(on_scalar, 1, HALF + CHUNK, CHUNK), 1, HALF + CHUNK, CHUNK)
+        nc.sync.dma_start(words_out[:, 1, HALF:], high_codes[1][:])
         for r in range(4):
             queue = nc.sync if r % 2 == 0 else nc.scalar
             queue.dma_start(

@@ -337,13 +337,15 @@ def tile_list_modal_operator_query_kernel(
         low_codes = late_tile([P, groups, HALF], I32, "low_codes", "trunk3")
         high_codes = [sb([P, HALF], I32, "high_codes%d" % g) for g in range(groups)]
         low = [weave(on_vector, g, 0, HALF, after) for g, after in enumerate(("c_bf4", "gated_rows"))]
-        for g, y_bf in enumerate(low):
-            quantise(low_codes[:, g, :], y_bf, g, 0, HALF)
-        nc.sync.dma_start(words_out[:, :, :HALF], low_codes[:])
+        quantise(low_codes[:, 0, :], low[0], 0, 0, HALF)
+        nc.sync.dma_start(words_out[:, 0, :HALF], low_codes[:, 0, :])
         third = weave(on_vector, 1, HALF, CHUNK)
-        upper = weave(on_vector, 0, HALF, HALF)
+        quantise(low_codes[:, 1, :], low[1], 1, 0, HALF)
+        nc.sync.dma_start(words_out[:, 1, :HALF], low_codes[:, 1, :])
         quantise(high_codes[1][:, :CHUNK], third, 1, HALF, CHUNK)
-        quantise(high_codes[0][:], upper, 0, HALF, HALF)
+        upper = [weave(on_vector, 0, HALF + u * CHUNK, CHUNK) for u in range(2)]
+        for u, y_bf in enumerate(upper):
+            quantise(high_codes[0][:, u * CHUNK : (u + 1) * CHUNK], y_bf, 0, HALF + u * CHUNK, CHUNK)
         nc.sync.dma_start(words_out[:, 0, HALF:], high_codes[0][:])
         quantise(high_codes[1][:, CHUNK:], weave(on_scalar, 1, HALF + CHUNK, CHUNK), 1, HALF + CHUNK, CHUNK)
         nc.sync.dma_start(words_out[:, 1, HALF:], high_codes[1][:])

@@ -185,8 +185,8 @@ def tile_list_modal_operator_query_kernel(
                     gate(t, first, CHUNK, resp[t][h][:, first : first + CHUNK])
             else:
                 gate(t, HALF, HALF, resp[t][h][:])
-        wb_sc = sb([P, KP], U8, "wb_sc", "resp1_0")
-        nc.vector.tensor_copy(
+        wb_sc = sb([P, KP], U8, "wb_sc")
+        nc.gpsimd.tensor_copy(
             wb_sc[:].rearrange("p (t m) -> p t m", t=PACK),
             wb_sc_raw[:].rearrange("p (m t) -> p t m", t=PACK),
         )

@@ -46,7 +46,7 @@ def tile_list_modal_operator_query_kernel(
         def sb(shape, dtype, name, after=None):
             return keep.tile(shape, dtype, name=name, tag=after or name, align_bytes=64)
 
-        places = {"trunk1": 0, "w2_first": 8192, "w2_second0": 16384, "trunk2": 20480, "w2_second1": 28672,
+        places = {"trunk1": 0, "w2_first": 8192, "trunk2": 16384, "w2_second0": 24576, "w2_second1": 28672,
                   "trunk3": 32768, "wb_raw0": 40960, "wb_raw1": 43008, "mean": 45056}
 
         def late_tile(shape, dtype, name, place=None):
@@ -151,8 +151,8 @@ def tile_list_modal_operator_query_kernel(
         mean = late_tile([P, groups, PACK], F32, "mean")
         nc.sync.dma_start(trunk[1][:], gT_rows[1])
         nc.sync.dma_start(w2_first[:], w2_rows[0])
-        nc.sync.dma_start(w2_second[0][:], w2_rows[1][:, :, : H // 2])
         nc.sync.dma_start(trunk[2][:], gT_rows[2])
+        nc.sync.dma_start(w2_second[0][:], w2_rows[1][:, :, : H // 2])
         nc.sync.dma_start(w2_second[1][:], w2_rows[1][:, :, H // 2 :])
         nc.sync.dma_start(trunk[3][:], gT_rows[3])
         wb_cols = wb_words[0].rearrange("p n i -> p (n i)").bitcast(I32)
@@ -179,7 +179,24 @@ def tile_list_modal_operator_query_kernel(
                 gated[part][:, t, j0 : j0 + count], trunk[t][:].indirect(list_cols(first, count)), response, MULT
             )
 
+        w2_codes, w2_sc = [], []
+
+        def quantise_w2(sources):
+            a = len(w2_codes)
+            grouped = sb([P, H * PACK], BF16, "w2_bf%d" % a)
+            dealt = grouped[:].rearrange("p (s e m i) -> p m s i e", s=2, e=2, i=PACK)
+            share = P // len(sources)
+            for u, raw in enumerate(sources):
+                nc.scalar.copy(
+                    dealt[:, u * share : (u + 1) * share], raw[:].rearrange("p i (m s e) -> p m s i e", s=2, e=2)
+                )
+            w2_codes.append(sb([P, H], U32, "w2_codes%d" % a))
+            w2_sc.append(sb([P, H], U8, "w2_sc%d" % a))
+            nc.vector.quantize_mx(w2_codes[a][:].bitcast(FP8X4), w2_sc[a][:], grouped[:])
+
         for h, t in in_order[: -len(held)]:
+            if (h, t) == (0, 2):
+                quantise_w2([w2_first])
             if h == 0:
                 for first in (0, CHUNK):
                     gate(t, first, CHUNK, resp[t][h][:, first : first + CHUNK])
@@ -191,18 +208,7 @@ def tile_list_modal_operator_query_kernel(
             wb_sc_raw[:].rearrange("p (m t) -> p t m", t=PACK),
         )
 
-        w2_codes, w2_sc = [], []
-        for a, sources in enumerate(([w2_first], w2_second)):
-            grouped = sb([P, H * PACK], BF16, "w2_bf%d" % a)
-            dealt = grouped[:].rearrange("p (s e m i) -> p m s i e", s=2, e=2, i=PACK)
-            share = P // len(sources)
-            for u, raw in enumerate(sources):
-                nc.scalar.copy(
-                    dealt[:, u * share : (u + 1) * share], raw[:].rearrange("p i (m s e) -> p m s i e", s=2, e=2)
-                )
-            w2_codes.append(sb([P, H], U32, "w2_codes%d" % a))
-            w2_sc.append(sb([P, H], U8, "w2_sc%d" % a))
-            nc.vector.quantize_mx(w2_codes[a][:].bitcast(FP8X4), w2_sc[a][:], grouped[:])
+        quantise_w2(w2_second)
 
         last_resp = []
         for (first, count), after in zip(parts, ("w2_second1", "w2_second0", "w2_first")):

from contextlib import ExitStack

import concourse.mybir as mybir

K, T, S, H, N = 1024, 2048, 1024, 512, 1024
FLOPS = 2 * (2 * K * H * S + H * N * S)

F32 = mybir.dt.float32
BF16 = mybir.dt.bfloat16
I32 = mybir.dt.int32
U32 = mybir.dt.uint32
U16 = mybir.dt.uint16
U8 = mybir.dt.uint8
FP8X4 = mybir.dt.float8_e4m3fn_x4
FP4X4 = mybir.dt.float4_e2m1fn_x4
ACT = mybir.ActivationFunctionType
MULT = mybir.AluOpType.mult

P = 128
PACK = 4
KP = P * PACK
QUADS = 4
BANK = 512
HALF = S // 2
BLOCK = BANK // PACK
CHUNK = 256
SPANS = ((0, BLOCK), (BLOCK, BLOCK), (CHUNK, CHUNK), (2 * CHUNK, CHUNK), (3 * CHUNK, CHUNK))
PAIR = BANK // CHUNK
W1_BANKS = 4
W2_BANKS = (4, 5, 6, 7, 2, 3, 4, 5)
Y_BANKS = (0, 1, 6, 7)


def tile_list_modal_operator_query_kernel(
    tc, tab_words, tab_scales, offs, gT, w1_words, w1_scales, b1, w2, wb_words, wb_scales, ymean, out_0, out_1, out_2
):
    nc = tc.nc
    passes = K // KP
    groups = N // KP

    with ExitStack() as ctx:
        keep = ctx.enter_context(tc.tile_pool(name="keep", bufs=1))
        late = ctx.enter_context(tc.tile_pool(name="late", bufs=1))
        psum = ctx.enter_context(tc.psum_pool(name="psum", bufs=1))

        def sb(shape, dtype, name, after=None):
            return keep.tile(shape, dtype, name=name, tag=after or name, align_bytes=64)

        places = {"trunk1": 0, "w2_first": 8192, "trunk2": 16384, "w2_second0": 24576, "w2_second1": 28672,
                  "trunk3": 32768, "wb_raw0": 40960, "wb_raw1": 43008, "mean": 45056}

        def late_tile(shape, dtype, name, place=None):
            place = place or name
            return late.tile(shape, dtype, name=name, tag=place, align_bytes=64, offset=places[place])

        def bank_tile(shape, bank):
            return psum.tile(shape, F32, name="sums", tag="bank%d" % bank)

        offsets = keep.tile([P, S // 16], U16, name="offsets")
        room = late.tile([P, places["mean"] + 64], U8, name="room", align_bytes=64, offset=0)
        tab_sc = room[:, :T]
        picked_sc = sb([P, S], U8, "picked_sc")
        moved_sc = sb([P, S], U8, "moved_sc")
        v_sc = [picked_sc, moved_sc]
        sc_raw = sb([P, passes * H], U8, "sc_raw")
        w1_raw = sb([P, passes * 2 * H], U8, "w1_raw")
        tab = [sb([P, T], I32, "tab%d" % a) for a in range(passes)]
        bias1 = sb([P, PACK], F32, "bias1")

        nc.gpsimd.memset(tab_sc[:112, :].bitcast(I32), 0)
        nc.vector.memset(sc_raw[:].bitcast(I32), 0)
        nc.vector.memset(moved_sc[:].bitcast(I32), 0)

        wb_sc_raw = sb([P, KP], U8, "wb_sc_raw")
        nc.gpsimd.memset(wb_sc_raw[:].bitcast(I32), 0)
        for q in range(QUADS):
            nc.gpsimd.dma_start(
                wb_sc_raw[32 * q + 8 : 32 * q + 16, :].bitcast(I32),
                wb_scales[0, 4 * q : 4 * q + 4, :].bitcast(I32).rearrange("r (g e) -> g r e", g=groups),
            )

        nc.sync.dma_start(offsets[:], offs)
        nc.sync.dma_start(
            w1_raw[:].bitcast(I32).rearrange("p (a n) -> p a n", a=passes),
            w1_words.bitcast(I32).rearrange("a p n -> p a n"),
        )
        nc.sync.dma_start(tab_sc[112:, :].bitcast(I32), tab_scales[1].bitcast(I32))
        for r in range(4):
            nc.sync.dma_start(tab_sc[r::32, :].bitcast(I32), tab_scales[0, r::4, :].bitcast(I32))
        nc.sync.dma_start(tab[0][:], tab_words[0].rearrange("p n i -> p (n i)").bitcast(I32))
        for r in range(4):
            nc.sync.dma_start(
                sc_raw[r::32, :].bitcast(I32).rearrange("q (a e) -> q a e", a=passes),
                w1_scales[:, r::4, :].bitcast(I32).rearrange("a q e -> q a e"),
            )
        nc.sync.dma_start(tab[1][:], tab_words[1].rearrange("p n i -> p (n i)").bitcast(I32))
        nc.sync.dma_start(bias1[:], b1.rearrange("(p t) -> p t", t=PACK))
        gT_rows = gT.rearrange("(p t) n -> t p n", t=PACK)
        trunk = [sb([P, T], F32, "trunk0")] + [late_tile([P, T], F32, "trunk%d" % t) for t in range(1, PACK)]
        nc.sync.dma_start(trunk[0][:], gT_rows[0])

        w1_codes = sb([P, passes * 2 * H], U8, "w1_codes")
        nc.vector.tensor_copy(
            w1_codes[:].bitcast(U16).rearrange("p (a t m) -> p a t m", a=passes, t=PACK),
            w1_raw[:].bitcast(U16).rearrange("p (a m t) -> p a t m", a=passes, t=PACK),
        )

        nc.vector.tensor_copy(picked_sc[:], tab_sc.indirect(offsets[:]))
        for r in range(4):
            nc.sync.dma_start(moved_sc[r::32, :].bitcast(I32), picked_sc[112 + r :: 4, :].bitcast(I32))

        def list_cols(first, count):
            return offsets[:, first // 16 : (first + count) // 16]

        v = [[sb([P, HALF], U32, "v%d_%d" % (a, h)) for h in range(2)] for a in range(passes)]
        nc.vector.tensor_copy(v[0][0][:], tab[0][:].bitcast(U32).indirect(list_cols(0, HALF)))
        w1_sc = sb([P, passes * H], U8, "w1_sc")
        nc.vector.tensor_copy(
            w1_sc[:].rearrange("p (a t m) -> p a t m", a=passes, t=PACK),
            sc_raw[:].rearrange("p (a m t) -> p a t m", a=passes, t=PACK),
        )
        nc.vector.tensor_copy(v[1][0][:], tab[1][:].bitcast(U32).indirect(list_cols(0, HALF)))
        for a in range(passes):
            nc.vector.tensor_copy(v[a][1][:], tab[a][:].bitcast(U32).indirect(list_cols(HALF, HALF)))

        resp = [[sb([P, HALF], F32, "resp%d_%d" % (t, h)) for h in range(2)] for t in range(PACK - 1)]
        held = []
        in_order = [(h, t) for h in range(2) for t in range(2)] + [(h, t) for t in (2, 3) for h in range(2)]
        for n, (h, t) in enumerate(in_order):
            acc = bank_tile([P, HALF], n % W1_BANKS)
            for a in range(passes):
                col = a * H + t * P
                nc.tensor.matmul_mx(
                    acc[:],
                    lhsT=w1_codes[:, 2 * col : 2 * (col + P)].bitcast(FP4X4),
                    lhsT_scale=w1_sc[:, col : col + P],
                    rhs=v[a][h][:].bitcast(FP8X4),
                    rhs_scale=v_sc[a][:, h * HALF : (h + 1) * HALF],
                    start=(a == 0),
                    stop=(a == passes - 1),
                )
            if t == PACK - 1:
                held.append(acc)
            else:
                nc.scalar.activation(resp[t][h][:], acc[:], ACT.Tanh, bias=bias1[:, t : t + 1])

        w2_rows = w2.rearrange("(a p i) r -> a p i r", a=passes, i=PACK)
        w2_first = late_tile([P, PACK, H], F32, "w2_first")
        w2_second = [late_tile([P, PACK, H // 2], F32, "w2_second%d" % u) for u in range(2)]
        wb_raw = [late_tile([P, KP], I32, "wb_raw%d" % g) for g in range(groups)]
        mean = late_tile([P, groups, PACK], F32, "mean")
        nc.sync.dma_start(trunk[1][:], gT_rows[1])
        nc.sync.dma_start(w2_first[:], w2_rows[0])
        nc.sync.dma_start(trunk[2][:], gT_rows[2])
        nc.sync.dma_start(w2_second[0][:], w2_rows[1][:, :, : H // 2])
        nc.sync.dma_start(w2_second[1][:], w2_rows[1][:, :, H // 2 :])
        nc.sync.dma_start(trunk[3][:], gT_rows[3])
        wb_cols = wb_words[0].rearrange("p n i -> p (n i)").bitcast(I32)
        for g in range(groups):
            nc.sync.dma_start(wb_raw[g][:], wb_cols[:, g * KP : (g + 1) * KP])
        nc.sync.dma_start(mean[:], ymean.rearrange("(g p t) -> p g t", g=groups, t=PACK))

        parts = ((0, CHUNK), (CHUNK, CHUNK), (HALF, HALF))
        second_at = (PACK - 1) * HALF + BLOCK
        first_at = second_at + PACK * CHUNK - BLOCK
        gated_rows = sb([P, first_at + PACK * CHUNK], F32, "gated_rows")
        gated = [
            gated_rows[:, base : base + PACK * count].rearrange("p (t j) -> p t j", t=PACK)
            for base, (first, count) in zip((first_at, second_at, 0), parts)
        ]

        def part_of(first):
            part = min(first // CHUNK, len(parts) - 1)
            return part, first - parts[part][0]

        def gate(t, first, count, response):
            part, j0 = part_of(first)
            nc.vector.tensor_tensor(
                gated[part][:, t, j0 : j0 + count], trunk[t][:].indirect(list_cols(first, count)), response, MULT
            )

        w2_codes, w2_sc = [], []

        def quantise_w2(sources):
            a = len(w2_codes)
            grouped = sb([P, H * PACK], BF16, "w2_bf%d" % a)
            dealt = grouped[:].rearrange("p (s e m i) -> p m s i e", s=2, e=2, i=PACK)
            share = P // len(sources)
            for u, raw in enumerate(sources):
                nc.scalar.copy(
                    dealt[:, u * share : (u + 1) * share], raw[:].rearrange("p i (m s e) -> p m s i e", s=2, e=2)
                )
            w2_codes.append(sb([P, H], U32, "w2_codes%d" % a))
            w2_sc.append(sb([P, H], U8, "w2_sc%d" % a))
            nc.vector.quantize_mx(w2_codes[a][:].bitcast(FP8X4), w2_sc[a][:], grouped[:])

        for h, t in in_order[: -len(held)]:
            if (h, t) == (0, 2):
                quantise_w2([w2_first])
            if h == 0:
                for first in (0, CHUNK):
                    gate(t, first, CHUNK, resp[t][h][:, first : first + CHUNK])
            else:
                gate(t, HALF, HALF, resp[t][h][:])
        wb_sc = sb([P, KP], U8, "wb_sc")
        nc.gpsimd.tensor_copy(
            wb_sc[:].rearrange("p (t m) -> p t m", t=PACK),
            wb_sc_raw[:].rearrange("p (m t) -> p t m", t=PACK),
        )

        quantise_w2(w2_second)

        last_resp = []
        for (first, count), after in zip(parts, ("w2_second1", "w2_second0", "w2_first")):
            last_resp.append(late_tile([P, count], F32, "last_resp%d" % first, after))
            j0 = first % HALF
            nc.scalar.activation(
                last_resp[-1][:], held[first // HALF][:, j0 : j0 + count], ACT.Tanh, bias=bias1[:, PACK - 1 :]
            )

        c_codes, c_sc, wb_codes = [], [], []

        def deal_wb(after):
            g = len(wb_codes)
            wb_codes.append(late_tile([P, KP], I32, "wb_codes%d" % g, after))
            nc.gpsimd.tensor_copy(
                wb_codes[g][:].rearrange("p (t m i) -> p m t i", t=PACK, i=4),
                wb_raw[g][:].rearrange("p (m i t) -> p m t i", t=PACK, i=4),
            )

        y = [sb([P, PACK, S], F32, "y%d" % g) for g in range(groups)]

        filled = []

        def y_bank(chunks, g, t0):
            first = SPANS[chunks[0]][0]
            width = sum(SPANS[chunk][1] for chunk in chunks)
            per_bank = BANK // width
            acc = bank_tile([P, per_bank, width], Y_BANKS[len(filled) % len(Y_BANKS)])
            filled.append(acc)
            for s in range(per_bank):
                col = (t0 + s) * P
                for chunk in chunks:
                    j0 = SPANS[chunk][0] - first
                    nc.tensor.matmul_mx(
                        acc[:, s, j0 : j0 + SPANS[chunk][1]],
                        lhsT=wb_codes[g][:, col : col + P].bitcast(FP8X4),
                        lhsT_scale=wb_sc[8 + 4 * g :, col : col + P],
                        rhs=c_codes[chunk][:].bitcast(FP8X4),
                        rhs_scale=c_sc[chunk][:],
                        start=True,
                        stop=True,
                    )
            for s in range(per_bank):
                t = t0 + s
                nc.scalar.activation(
                    y[g][:, t, first : first + width], acc[:, s, :], ACT.Identity, bias=mean[:, g, t : t + 1]
                )

        def store(queue, g, t0, t1, first, width):
            rows = out_0[g * KP : (g + 1) * KP, first : first + width].rearrange("(p t) j -> p t j", t=PACK)
            queue.dma_start(rows[:, t0:t1, :], y[g][:, t0:t1, first : first + width])

        y_sc = sb([P, groups * S], U8, "y_sc")
        words_out = out_1.rearrange("g p j t -> p g (j t)").bitcast(I32)

        def weave(engine_copy, g, first, width, after=None):
            y_bf = sb([P, width, PACK], BF16, "y_bf%d_%d" % (first, g), after)
            engine_copy(
                y_bf[:].rearrange("p (c i) t -> p c t i", i=4),
                y[g][:, :, first : first + width].rearrange("p t (c i) -> p c t i", i=4),
            )
            return y_bf

        def quantise(codes, y_bf, g, first, width):
            nc.vector.quantize_mx(
                codes.bitcast(FP8X4),
                y_sc[:, g * S + first : g * S + first + width],
                y_bf[:].rearrange("p j t -> p (j t)"),
            )

        for chunk, (first, width) in enumerate(SPANS):
            h = first // HALF
            part, in_part = part_of(first)
            narrow = width == BLOCK
            if first == 0:
                for j0 in (0, BLOCK):
                    gate(PACK - 1, j0, BLOCK, last_resp[0][:, j0 : j0 + BLOCK])
                deal_wb("w2_second1")
            if not narrow:
                gate(PACK - 1, first, width, last_resp[part][:, in_part : in_part + width])
            if first == CHUNK:
                deal_wb("w2_second0")
            c_bf = sb([P, width, PACK], BF16, "c_bf%d" % chunk)
            for w in range(width // BLOCK):
                j0 = first % HALF + w * BLOCK
                j1 = in_part + w * BLOCK
                lin = bank_tile([P, PACK, BLOCK], W2_BANKS[first // BLOCK + w])
                for a in range(passes):
                    for t in range(PACK):
                        nc.tensor.matmul_mx(
                            lin[:, t, :],
                            lhsT=w2_codes[a][:, t * P : (t + 1) * P].bitcast(FP8X4),
                            lhsT_scale=w2_sc[a][:, t * P : (t + 1) * P],
                            rhs=v[a][h][:, j0 : j0 + BLOCK].bitcast(FP8X4),
                            rhs_scale=v_sc[a][:, h * HALF + j0 : h * HALF + j0 + BLOCK],
                            start=(a == 0 and t == 0),
                            stop=(a == passes - 1 and t == PACK - 1),
                        )
                nc.vector.tensor_tensor(
                    c_bf[:, w * BLOCK : (w + 1) * BLOCK, :].rearrange("p (c i) t -> p c t i", i=4),
                    lin[:].rearrange("p t (c i) -> p c t i", i=4),
                    gated[part][:, :, j1 : j1 + BLOCK].rearrange("p t (c i) -> p c t i", i=4),
                    MULT,
                )
            c_codes.append(sb([P, width], U32, "c_codes%d" % chunk))
            c_sc.append(sb([P, width], U8, "c_sc%d" % chunk))
            nc.vector.quantize_mx(
                c_codes[chunk][:].bitcast(FP8X4), c_sc[chunk][:], c_bf[:].rearrange("p j t -> p (j t)")
            )
            if narrow:
                y_bank([chunk], 0, 0)
                store(nc.sync, 0, 0, PACK, first, width)
            if first == CHUNK:
                for chunks, g, start in (([0, 1], 1, 0), ([2], 0, CHUNK)):
                    for t0 in range(0, PACK, PAIR):
                        y_bank(chunks, g, t0)
                        store(nc.sync, g, t0, t0 + PAIR, start, CHUNK)
                y_bank([2], 1, 0)
                store(nc.sync, 1, 0, PAIR, CHUNK, CHUNK)
                y_bank([2], 1, PAIR)

        y_bank([3], 1, PAIR)
        store(nc.sync, 1, PAIR, PACK, CHUNK, HALF)
        for g, t0, queue in ((1, 0, nc.sync), (0, 0, nc.scalar), (0, PAIR, nc.scalar)):
            y_bank([3], g, t0)
            y_bank([4], g, t0)
            store(queue, g, t0, t0 + PAIR, HALF, HALF)
        y_bank([4], 1, PAIR)
        store(nc.scalar, 1, PAIR, PACK, HALF + CHUNK, CHUNK)

        on_vector, on_scalar = nc.vector.tensor_copy, nc.scalar.copy
        low_codes = late_tile([P, groups, HALF], I32, "low_codes", "trunk3")
        high_codes = [sb([P, HALF], I32, "high_codes%d" % g) for g in range(groups)]
        low = [weave(on_vector, g, 0, HALF, after) for g, after in enumerate(("c_bf4", "gated_rows"))]
        quantise(low_codes[:, 0, :], low[0], 0, 0, HALF)
        nc.sync.dma_start(words_out[:, 0, :HALF], low_codes[:, 0, :])
        third = weave(on_vector, 1, HALF, CHUNK)
        quantise(low_codes[:, 1, :], low[1], 1, 0, HALF)
        nc.sync.dma_start(words_out[:, 1, :HALF], low_codes[:, 1, :])
        quantise(high_codes[1][:, :CHUNK], third, 1, HALF, CHUNK)
        upper = [weave(on_vector, 0, HALF + u * CHUNK, CHUNK) for u in range(2)]
        for u, y_bf in enumerate(upper):
            quantise(high_codes[0][:, u * CHUNK : (u + 1) * CHUNK], y_bf, 0, HALF + u * CHUNK, CHUNK)
        nc.sync.dma_start(words_out[:, 0, HALF:], high_codes[0][:])
        quantise(high_codes[1][:, CHUNK:], weave(on_scalar, 1, HALF + CHUNK, CHUNK), 1, HALF + CHUNK, CHUNK)
        nc.sync.dma_start(words_out[:, 1, HALF:], high_codes[1][:])
        for r in range(4):
            queue = nc.sync if r % 2 == 0 else nc.scalar
            queue.dma_start(
                out_2[:, r::4, :].bitcast(I32).rearrange("g q j -> q g j"),
                y_sc[r::32, :].bitcast(I32).rearrange("q (g j) -> q g j", g=groups),
            )
